import numpy as np, ml_dtypes
CORES = [2,3,42,43,82,83,122,123]
N = 8
BF = ml_dtypes.bfloat16
def f(rng, *shape):
    return (rng.standard_normal(shape, dtype=np.float32) * np.exp2(rng.integers(-2, 3, shape[:-1] + (1,)))).astype(BF)
def wide(rng, *shape):
    v = f(rng, *shape).astype(np.float32); k = shape[:-2] + (1, shape[-1])
    return (v * np.exp2(rng.integers(-6, 7, k)) * (rng.random(k) > 0.0625)).astype(BF)
def gentries(a):
    return np.ascontiguousarray(a.reshape(8, 16, -1).transpose(0, 2, 1)).reshape(8, -1)
def gtable(e):
    e = np.asarray(e); return np.ascontiguousarray(e.reshape(8, -1, 16).transpose(0, 2, 1)).reshape(128, -1).astype(np.int32)
WAY = "abc"; W = len(WAY)
IC, CG, CAPP, TOT, S = 2048, 256, 256, 2048, 512
def numbers(a):
    return np.stack([gentries(u) for u in a])
def slots(a):
    return np.stack([gentries(u) for u in a]).reshape(N, N, CAPP)
def columns(t, a):
    e = slots(a); t = t.astype(np.float64)
    return np.stack([np.concatenate([t[q][:, e[q, r]] for q in range(N)], axis=1) for r in range(N)])
def sums(t, x):
    return np.stack([np.bincount(x, weights=t[o], minlength=TOT) for o in range(16)])
def home(p, a):
    e = slots(a); y = np.zeros((N, 16, IC), np.float64)
    for q in range(N):
        for r in range(N):
            y[q][:, e[q, r]] += p[r][:, q * CAPP:(q + 1) * CAPP]
    return y
def anyslots(rng):
    return np.argsort(rng.random((W, N, N, IC)), axis=-1)[..., :CAPP]
def anynumbers(rng):
    x = rng.integers(0, TOT, (W, N, 8, S)); few = rng.integers(0, TOT, (W, N, 8, 32))
    return np.where(rng.random(x.shape) < 0.5, np.take_along_axis(few, rng.integers(0, 32, x.shape), axis=-1), x)
def make(rng, x, e):
    o = np.argsort(x[0], axis=-1, kind="stable"); x = np.stack([np.take_along_axis(u, o, axis=-1) for u in x])
    ob = np.lexsort((rng.random(x[1].shape), x[1]), axis=-1)
    d = {"f" + c: f(rng, N, 16, IC) for c in WAY}
    d["v"] = (rng.standard_normal((N, 8, S)) * np.exp2(rng.integers(-1, 2, (N, 8, 1)))).astype(np.float32)
    for w, c in enumerate(WAY): d["x" + c] = np.stack([gtable(u) for u in x[w]])
    d["ob"] = np.stack([gtable(u) for u in ob])
    for w, c in enumerate(WAY): d["l" + c] = np.stack([gtable(u.reshape(8, CG)) for u in e[w]])
    return d
def setup_inputs(rng):
    return make(rng, anynumbers(rng), anyslots(rng))
def setup_inputs_runs(rng):
    x = anynumbers(rng); h = rng.integers(0, TOT, (W, N, 8, 1))
    for w in range(W): x[w, :, :, w * S // 8:w * S // 8 + S // 2] = h[w]
    x[0, :, 0:2] = h[0, :, 0:1]; x[1, :, 1:3] = h[1, :, 1:2]
    return make(rng, x, anyslots(rng))
def setup_inputs_apart(rng):
    x = np.argsort(rng.random((W, N, 8 * S // TOT, TOT)), axis=-1).reshape(W, N, 8, S)
    return make(rng, x, anyslots(rng))
def setup_inputs_ends(rng):
    x = rng.integers(0, N, (W, N, 8, S)) * CAPP + rng.integers(0, 2, (W, N, 8, S)) * (CAPP - 1)
    x = np.where(rng.random(x.shape) < 0.75, x, rng.integers(0, TOT, x.shape)); x[..., 0] = 0; x[..., 1] = TOT - 1
    e = 1 + np.argsort(rng.random((W, N, N, IC - 2)), axis=-1)[..., :CAPP]; e[..., 0] = IC - 1; e[..., -1] = 0
    return make(rng, x, e)
def setup_inputs_alike(rng):
    x = anynumbers(rng); x[:, :, 1:] = x[:, :, :1].copy()
    e = np.repeat(np.argsort(rng.random((W, N, 1, IC)), axis=-1)[..., :CAPP], N, axis=2)
    return make(rng, x, e)
def setup_inputs_spread(rng):
    d = setup_inputs(rng)
    for c in WAY[1:]: d["f" + c] = wide(rng, N, 16, IC)
    return d
def check_inputs(d):
    bad = []
    for c in WAY:
        x = numbers(d["x" + c]); e = slots(d["l" + c])
        if not np.isfinite(d["f" + c].astype(np.float32)).all(): bad.append("finite_f" + c)
        if x.min() < 0 or x.max() >= TOT: bad.append("range_x" + c)
        if e.min() < 0 or e.max() >= IC: bad.append("range_l" + c)
        if (np.diff(np.sort(e, axis=-1), axis=-1) == 0).any(): bad.append("different_l" + c)
    if not np.isfinite(d["v"]).all(): bad.append("finite_v")
    if (np.diff(numbers(d["xa"]), axis=-1) < 0).any(): bad.append("sorted_xa")
    o = numbers(d["ob"])
    if not (np.sort(o, axis=-1) == np.arange(S)).all(): bad.append("places_ob")
    elif (np.diff(np.take_along_axis(numbers(d["xb"]), o, axis=-1), axis=-1) < 0).any(): bad.append("sorted_xb_by_ob")
    return bad
def reference(fa, fb, fc, v, xa, xb, xc, ob, la, lb, lc):
    xi = numbers(xa).reshape(N, 8 * S); xj = numbers(xb).reshape(N, 8 * S)
    w = np.repeat(v.astype(np.float64).reshape(N, 1, 8 * S), 16, axis=1)
    for t, x, a in ((fc, xc, lc),):
        u = columns(t, a); x = numbers(x).reshape(N, 8 * S)
        w = w * np.stack([u[r][:, x[r]] for r in range(N)])
    u = columns(fb, lb)
    ya = fa.astype(np.float64) * home([sums(w[r] * u[r][:, xj[r]], xi[r]) for r in range(N)], la)
    u = columns(ya, la)
    yb = home([sums(w[r] * u[r][:, xi[r]], xj[r]) for r in range(N)], lb)
    return {"ya": ya.astype(np.float32), "yb": yb.astype(np.float32)}

@@ -1,0 +1,457 @@
+import numpy as np
+from concourse.bass import DstId, RemoteDMATransfer
+from concourse.mybir import AluOpType, ActivationFunctionType
+
+OPS = AluOpType
+COPY = ActivationFunctionType.Copy
+F, BFT, I32, U16 = "float32", "bfloat16", "int32", "uint16"
+
+NDUMP = 640
+SCRATCH = {}
+for _n, _c, _t in [
+        ("i1", 128, I32), ("i1b", 128, I32), ("i2", 8, I32), ("i2b", 8, I32), ("i3", 128, I32), ("i4", 128, I32),
+        ("i4b", 128, I32), ("i5", 128, I32), ("ki", 32, I32), ("kk", 32, U16), ("dj", 32, F),
+        ("mk", 8, F), ("i16", 512, F), ("z", 240, F), ("ident", 128, F), ("mbf", 128, F), ("mbb", 128, BFT),
+        ("e8", 128, F), ("rm", 4, F), ("n1", 128, F), ("n2", 128, F), ("p1", 128, F), ("p2", 128, F),
+        ("repb", 1024, BFT), ("repf", 1024, F),
+        ("tf", 4096, BFT), ("far", 2048, BFT), ("v8", 512, F), ("v16", 512, F), ("xi", 128, I32), ("ln", 32, I32),
+        ("lau", 16, U16), ("lbu", 16, U16), ("lu", 32, U16), ("lta", 16, U16),
+        ("t1", 64, I32), ("t2", 64, I32), ("t3", 64, I32), ("t4", 64, I32), ("t5", 64, I32), ("xu", 64, U16),
+        ("obu", 32, U16), ("xpa", 34, F), ("xpb", 34, F),
+        ("ea", 32, F), ("ca", 32, F), ("da", 32, F), ("fma", 32, F), ("ga", 32, F), ("offa", 32, U16),
+        ("eb", 32, F), ("cb", 32, F), ("db", 32, F), ("fmb", 32, F), ("gb", 32, F), ("offb", 32, U16),
+        ("exa", 512, BFT), ("exb", 512, BFT), ("ma", 512, F), ("mb", 512, F),
+        ("pk0", 32, F), ("pk", 32, F), ("exp", 512, F), ("fp", 512, F), ("pm", 512, F), ("pint", 32, I32),
+        ("xao", 32, I32), ("xbo", 32, I32), ("u1", 32, I32), ("u2", 32, I32), ("u3", 32, I32), ("u4", 32, I32),
+        ("u5", 32, I32), ("xaou", 32, U16),
+        ("s1", 512, BFT), ("tb", 2048, BFT), ("tc", 2048, BFT), ("vc", 512, F), ("vcp", 512, F), ("wa", 512, F),
+        ("ra", 512, F), ("w1", 2048 + NDUMP, F), ("s3", 256, F), ("q3", 256, F), ("w2", 2048, F), ("yat", 2048, F),
+        ("s5", 256, F), ("land3", 256, F), ("land5", 256, F), ("land6", 256, F), ("ta", 2048, F), ("wb", 512, F),
+        ("rb", 512, F), ("w3", 2048 + NDUMP, F), ("s6", 256, F), ("q6", 256, F), ("w4", 2048, F), ("ybt", 2048, F)]:
+    SCRATCH[_n] = ("sbuf", [128, _c], _t)
+SCRATCH["ll"] = ("sbuf", [128, 3, 8, 2], I32)
+SCRATCH["llf"] = ("sbuf", [128, 8, 4], F)
+SCRATCH["laf"] = ("sbuf", [128, 8, 2], F)
+SCRATCH["rr"] = ("sbuf", [128, 8, 8, 4], F)
+SCRATCH["rra"] = ("sbuf", [128, 8, 8, 2], F)
+SCRATCH["land1"] = ("sbuf", [128, 16, 32], BFT)
+for _k in range(8):
+    SCRATCH["ps%d" % _k] = ("psum", [128, 512], F)
+NSEM = 140
+SEMAPHORES = ["e%d" % k for k in range(NSEM)] + ["arr1", "arr3", "arr5", "arr6", "sent"]
+
+
+def rank_program(g, core, T, topo):
+    me = T.rank_of(core)
+    if me is None:
+        return
+    cores = list(T.cores)
+    here = topo.chip(core)
+    queues = {"v": g.vector, "s": g.scalar, "t": g.tensor, "g": g, "y": g.sync}
+
+    ops = []
+    hist = {}
+    groups = {}
+
+    def record(q, f, outs, ins, grp=None, inc=1, fixed=None):
+        k = len(ops)
+        dep = set()
+        touched = []
+        for w, side in ((1, outs), (0, ins)):
+            for pair in side:
+                for reg in pair[1]:
+                    touched.append((w, reg))
+        for w, reg in touched:
+            n, a, b, lo, hi = reg
+            for (j, w2, a2, b2, lo2, hi2) in hist.get(n, []):
+                if n[:2] == "ps":
+                    if ops[j]["q"] == q:
+                        if q != "t" and (w or w2) and lo < hi2 and lo2 < hi:
+                            dep.add(j)
+                    else:
+                        dep.add(j)
+                elif (w or w2) and lo < hi2 and lo2 < hi and a < b2 and a2 < b:
+                    dep.add(j)
+        for w, reg in touched:
+            hist.setdefault(reg[0], []).append((k, w) + tuple(reg[1:]))
+        if grp is not None:
+            groups.setdefault(grp, []).append(k)
+        dep.discard(k)
+        ops.append({"q": q, "f": f, "dep": dep, "grp": grp, "inc": inc, "fixed": fixed})
+        return k
+
+    def A(n, lo=0, hi=None, p0=0, p1=128, step=1):
+        hi = SCRATCH[n][1][1] if hi is None else hi
+        return (T[n][p0:p1, lo:hi] if step == 1 else T[n][p0:p1, lo:hi:step], [(n, p0, p1, lo, hi)])
+
+    def X(ap, n, lo, hi):
+        return (ap, [(n, 0, 128, lo, hi)])
+
+    def ind(win, off):
+        return (win[0].indirect(off[0]), win[1] + off[1])
+
+    def cp(q, out, in_, grp=None):
+        if q == "v":
+            record(q, lambda: g.vector.tensor_copy(out[0], in_[0]), [out], [in_], grp)
+        else:
+            record(q, lambda: g.scalar.activation(out[0], in_[0], COPY), [out], [in_], grp)
+
+    def scaled(out, in_, s, grp=None):
+        if isinstance(s, tuple):
+            record("s", lambda: g.scalar.activation(out[0], in_[0], COPY, scale=s[0]), [out], [in_, s], grp)
+        else:
+            record("s", lambda: g.scalar.activation(out[0], in_[0], COPY, scale=s), [out], [in_], grp)
+
+    def tt(out, a, b, o, grp=None):
+        record("v", lambda: g.vector.tensor_tensor(out[0], a[0], b[0], o), [out], [a, b], grp)
+
+    def ts(out, a, s1, o1, s2=None, o2=None, grp=None):
+        ins = [a] + [s for s in (s1, s2) if isinstance(s, tuple)]
+        v1 = s1[0] if isinstance(s1, tuple) else s1
+        v2 = s2[0] if isinstance(s2, tuple) else s2
+        if o2 is None:
+            record("v", lambda: g.vector.tensor_scalar(out[0], a[0], v1, None, o1), [out], ins, grp)
+        else:
+            record("v", lambda: g.vector.tensor_scalar(out[0], a[0], v1, v2, o1, o2), [out], ins, grp)
+
+    def fill(out, c, grp=None):
+        record("v", lambda: g.vector.memset(out[0], c), [out], [], grp)
+
+    def mm(out, l, r, start, stop, grp):
+        record("t", lambda: g.tensor.matmul(out[0], l[0], r[0], start, stop), [out], [l, r], grp)
+
+    def iota(n, cols, pattern, base, cm, fl=False):
+        out = A(n, 0, cols)
+        if fl:
+            record("g", lambda: g.iota(out[0], pattern, base, cm, allow_small_or_imprecise_dtypes=True), [out], [])
+        else:
+            record("g", lambda: g.iota(out[0], pattern, base, cm), [out], [])
+
+    def dma(q, out, in_, grp):
+        e = queues[q]
+        record(q, lambda: e.dma_start(out[0], in_[0]), [out], [in_], grp, 16)
+
+    def ext(ap, n):
+        return (ap, [("ext_" + n, 0, 128, 0, 1)])
+
+    sib = [q for q in range(len(cores)) if q != me and topo.chip(cores[q]) == here]
+    near = [q for q in range(len(cores)) if topo.same_plane(topo.chip(cores[q]), here)]
+    far = [q for q in range(len(cores)) if q != me and q not in sib and q not in near]
+    order = far + near + sib + [me]
+
+    def share(q, dests, engines):
+        n = len(engines) // len(dests)
+        i = dests.index(q)
+        return engines[i * n:(i + 1) * n]
+
+    off_chip = topo.engines(core, cores[far[0]])
+    on_chip = [e for e in topo.engines(core, cores[sib[0]]) if e not in off_chip]
+
+    def engines_for(q):
+        if q in far:
+            return share(q, far, off_chip)
+        if q in near:
+            return share(q, near, off_chip)
+        return on_chip[:len(on_chip) // 2]
+
+    n_in = sum(len(engines_for(q)) for q in far + near + sib)
+    sent = [0]
+
+    def send(dests, src, width, dst, arr):
+        tr, rd = [], []
+        for q in dests:
+            d = order.index(q)
+            s = A(src, d * width, (d + 1) * width)
+            rd.append(s)
+            rid, pid = topo.addr(cores[q])[:2]
+            es = engines_for(q)
+            sent[0] += len(es)
+            tr.append(RemoteDMATransfer(dst_ids=[DstId(rid=rid, pnc=pid)], dma_engine_mask=sum(1 << e for e in es),
+                                        remote_sem=T.sem[arr], srcs=[s[0]], dsts=[dst(me)]))
+        record("g", lambda: g.remote_dma_fused(tr, local_sem=T.sem["sent"]), [], rd)
+
+    def arrival(n, width, arr):
+        regs = [(n, 0, 128, q * width, (q + 1) * width) for q in range(len(cores)) if q != me]
+        record("in_" + arr, None, [(None, regs)], [], fixed=(arr, n_in))
+
+    dma("y", X(T["ll"][:, 0, :, :], "ll", 0, 16), ext(T["lb"][:, :], "lb"), "d_l")
+    dma("y", X(T["ll"][:, 1, :, :], "ll", 16, 32), ext(T["lc"][:, :], "lc"), "d_l")
+    for k in range(8):
+        dma("y", A("tf", 0, 2048, 16 * k, 16 * k + 16), ext(T["fb"][:, :], "fb"), "d_tf")
+        dma("s", A("tf", 2048, 4096, 16 * k, 16 * k + 16), ext(T["fc"][:, :], "fc"), "d_tf")
+    for k, n in enumerate(("xa", "xb", "xc", "ob")):
+        dma("y", A("xi", 32 * k, 32 * k + 32), ext(T[n][:, :], n), "d_x")
+    dma("y", A("v8", 0, 512, 0, 8), ext(T["v"][:, :], "v"), "d_x")
+    dma("y", X(T["ll"][:, 2, :, :], "ll", 32, 48), ext(T["la"][:, :], "la"), "d_x")
+    dma("y", A("ln", 0, 16), ext(T["la"][:, :], "la"), "d_x")
+    dma("y", A("ln", 16, 32), ext(T["lb"][:, :], "lb"), "d_x")
+    for k in range(8):
+        dma("y", A("far", 0, 2048, 16 * k, 16 * k + 16), ext(T["fa"][:, :], "fa"), "d_fa")
+
+    iota("i2", 8, [[-16, 8]], 0, 1)
+    iota("i1", 128, [[0, 8], [-1, 16]], 16, 1)
+    iota("ki", 32, [[1, 32]], 0, 0)
+    iota("i3", 128, [[-1, 128]], 0, 1)
+    iota("i4", 128, [[-16, 8], [0, 16]], 0, 1)
+    iota("i5", 128, [[1, 8], [0, 16]], 0, -1)
+    iota("dj", 32, [[16, 32]], 2048, 1, True)
+    fill(A("z"), 0.0)
+    fill(A("xpa"), -1.0)
+    fill(A("xpb"), -1.0)
+    ts(A("i2b"), A("i2"), 4, OPS.arith_shift_right)
+    ts(A("mk"), A("i2b"), 0, OPS.is_equal)
+    ts(A("i1b"), A("i1"), 15, OPS.bitwise_and)
+    ts(A("i16", 0, 128), A("i1b"), 0, OPS.is_equal)
+    cp("v", A("z", 112, 128), A("i16", 0, 16))
+
+    ll, llf, rr = T["ll"], T["llf"], T["rr"]
+    cp("v", X(llf[:, :, 0:2], "llf", 0, 1), X(ll[:, 0, :, :], "ll", 0, 16))
+    ts(X(llf[:, :, 2:4], "llf", 1, 2), X(ll[:, 1, :, :], "ll", 16, 32), 2048, OPS.add)
+    for d in range(8):
+        r = order[d]
+        ts(X(rr[:, :, d, :], "rr", d, d + 1), X(llf[:, :, :], "llf", 0, 2), A("mk", r, r + 1), OPS.mult, grp="g_rr")
+    for h in range(8):
+        mm(A("ps0", 0, 32), A("z", 112 - 16 * h, 240 - 16 * h), X(rr[:, h, :, :], "rr", 0, 8), h == 0, h == 7, "g_lt")
+    cp("v", A("lu"), A("ps0", 0, 32))
+    cp("v", A("s1", 0, 256), ind(A("tf"), A("lu", 0, 16)))
+    cp("s", A("s1", 256, 512), ind(A("tf"), A("lu", 16, 32)))
+
+    land1 = T["land1"]
+
+    def at1(q):
+        return land1[:, 2 * q:2 * q + 2, :]
+
+    send(far, "s1", 64, at1, "arr1")
+    send(near + sib, "s1", 64, at1, "arr1")
+    for f in range(2):
+        cp("s", X(land1[:, 2 * me + f, :], "land1", 2 * me + f, 2 * me + f + 1),
+           A("s1", 448 + 32 * f, 480 + 32 * f), "g_own1")
+
+    for h in range(8):
+        scaled(A("repb", 128 * h, 128 * h + 128), A("i16", 0, 128), A("mk", h, h + 1), "g_repb")
+    for k in range(1, 4):
+        cp("s", A("i16", 128 * k, 128 * k + 128), A("i16", 0, 128), "g_i16")
+    cp("v", A("kk"), A("ki"))
+    ts(A("i4b"), A("i4"), 4, OPS.arith_shift_right)
+    ts(A("mbb"), A("i4b"), 0, OPS.is_equal)
+    ts(A("mbf"), A("i4b"), 0, OPS.is_equal)
+    ts(A("e8"), A("i5"), 0, OPS.is_equal)
+    mm(A("ps1"), A("e8", 0, 128, 0, 8), A("v8", 0, 512, 0, 8), True, True, "g_v")
+    cp("s", A("v16"), A("ps1"))
+
+    cp("v", A("rm", 0, 1), A("i16", 0, 1))
+    cp("v", A("rm", 1, 2), A("i16", 15, 16))
+    ts(A("rm", 2, 3), A("i16", 0, 1), -1.0, OPS.mult, 1.0, OPS.add)
+    ts(A("rm", 3, 4), A("i16", 15, 16), -1.0, OPS.mult, 1.0, OPS.add)
+    cp("v", A("xpa", 1, 33), A("xi", 0, 32))
+    ts(A("n1"), A("i3"), 1, OPS.is_equal, A("rm", 2, 3), OPS.mult, grp="g_sh")
+    ts(A("n2"), A("i3"), -15, OPS.is_equal, A("rm", 0, 1), OPS.mult, grp="g_sh")
+    ts(A("p1"), A("i3"), -1, OPS.is_equal, A("rm", 3, 4), OPS.mult, grp="g_sh")
+    ts(A("p2"), A("i3"), 15, OPS.is_equal, A("rm", 1, 2), OPS.mult, grp="g_sh")
+
+    def runs(xp, ps, s, off, ex):
+        mm(A(ps, 0, 32), A("n1"), A(xp, 1, 33), True, False, "g_n" + s)
+        mm(A(ps, 0, 32), A("n2"), A(xp, 2, 34), False, True, "g_n" + s)
+        mm(A(ps, 32, 64), A("p1"), A(xp, 1, 33), True, False, "g_n" + s)
+        mm(A(ps, 32, 64), A("p2"), A(xp, 0, 32), False, True, "g_n" + s)
+        tt(A("d" + s), A(xp, 1, 33), A("dj"), OPS.subtract)
+        tt(A("c" + s), A(ps, 32, 64), A(xp, 1, 33), OPS.is_equal)
+        tt(A("e" + s), A(ps, 0, 32), A(xp, 1, 33), OPS.not_equal)
+        tt(A(ex), ind(A("c" + s), A("kk")), A("i16"), OPS.mult)
+        tt(A("fm" + s), A("d" + s), A("e" + s), OPS.mult)
+        tt(A("g" + s), A("fm" + s), A("dj"), OPS.add)
+        cp("v", A(off), A("g" + s))
+
+    def slots(x, n, t, out):
+        ts(A(t[0], 0, n), x, 5, OPS.arith_shift_right, 7, OPS.bitwise_and)
+        ts(A(t[1], 0, n), x, 8, OPS.arith_shift_right)
+        tt(A(t[2], 0, n), A(t[0], 0, n), A(t[1], 0, n), OPS.subtract)
+        ts(A(t[3], 0, n), A(t[2], 0, n), 224, OPS.mult)
+        tt(A(t[4], 0, n), A(t[3], 0, n), x, OPS.add)
+        cp("v", out, A(t[4], 0, n))
+
+    runs("xpa", "ps7", "a", "offa", "exa")
+    mm(A("ps6"), A("mbb"), A("exa"), True, True, "g_ma")
+    cp("s", A("ma"), A("ps6"))
+    slots(A("xi", 32, 96), 64, ("t1", "t2", "t3", "t4", "t5"), A("xu"))
+    fill(A("w1", 0, 2048), 0.0)
+    scaled(A("w2"), A("tf", 0, 2048), 0.0)
+    ts(A("ident"), A("i3"), 0, OPS.is_equal)
+
+    arrival("land1", 2, "arr1")
+    for f, first in ((1, 0), (0, 4)):
+        for h in range(8):
+            mm(A("ps%d" % (first + h // 2), 256 * (h % 2), 256 * (h % 2) + 256), A("repb", 128 * h, 128 * h + 128),
+               X(land1[:, f::2, :], "land1", 0, 16), True, True, "g_t%d%d" % (f, h // 2))
+    for k in range(4):
+        cp("vs"[k % 2], A("tc", 512 * k, 512 * k + 512), A("ps%d" % k))
+    for k in range(3):
+        cp("s", A("tb", 512 * k, 512 * k + 512), A("ps%d" % (4 + k)))
+    tt(A("vc"), ind(A("tc"), A("xu", 32, 64)), A("v16"), OPS.mult)
+    cp("v", A("tb", 1536, 2048), A("ps7"))
+    tt(A("wa"), ind(A("tb"), A("xu", 0, 32)), A("vc"), OPS.mult)
+    record("v", lambda: g.vector.tensor_tensor_scan(T["ra"][:, :], T["ma"][:, :], T["wa"][:, :], 0.0, OPS.mult, OPS.add),
+           [A("ra")], [A("ma"), A("wa")])
+    cp("v", ind(A("w1"), A("offa")), A("ra"))
+
+    def add_slabs(w, s, land, arr):
+        for d in range(8):
+            for b in range(2):
+                c = 32 * (d % 4)
+                k = 2 * order[d] + b
+                mm(A("ps0" if d < 4 else "ps1", c + b, c + 32, step=2), A(w, 128 * k, 128 * k + 128), A("i16", 0, 16),
+                   True, True, "g_%s%d" % (w, d // 4))
+        cp("v", A(s, 0, 128), A("ps0", 0, 128))
+        cp("s", A(s, 128, 256), A("ps1", 0, 128))
+
+        def at(q):
+            return T[land][:, 32 * q:32 * q + 32]
+
+        send(far, s, 32, at, arr)
+        send(near + sib, s, 32, at, arr)
+        cp("s", A(land, 32 * me, 32 * me + 32), A(s, 224, 256))
+
+    add_slabs("w1", "s3", "land3", "arr3")
+
+    cp("v", A("lau"), A("ln", 0, 16))
+    cp("v", A("lbu"), A("ln", 16, 32))
+    laf, rra = T["laf"], T["rra"]
+    cp("v", X(laf[:, :, :], "laf", 0, 1), X(ll[:, 2, :, :], "ll", 32, 48))
+    for d in range(8):
+        r = order[d]
+        ts(X(rra[:, :, d, :], "rra", d, d + 1), X(laf[:, :, :], "laf", 0, 1), A("mk", r, r + 1), OPS.mult, grp="g_rra")
+    for h in range(8):
+        mm(A("ps4", 0, 16), A("z", 112 - 16 * h, 240 - 16 * h), X(rra[:, h, :, :], "rra", 0, 8), h == 0, h == 7, "g_lta")
+    cp("v", A("obu"), A("xi", 96, 128))
+    ts(A("pk0"), A("xi", 32, 64), 2048, OPS.mult)
+    tt(A("pk"), A("pk0"), A("xpa", 1, 33), OPS.add)
+    tt(A("exp"), ind(A("pk"), A("kk")), A("i16"), OPS.mult)
+    cp("v", A("lta"), A("ps4", 0, 16))
+    mm(A("ps2"), A("mbf"), A("exp"), True, True, "g_fp")
+    cp("s", A("fp"), A("ps2"))
+    cp("s", A("vcp"), ind(A("vc"), A("obu")))
+    tt(A("pm"), ind(A("fp"), A("obu")), A("i16"), OPS.mult)
+    for i in range(16):
+        mm(A("ps3", 0, 32), A("ident"), A("pm", i, 512, step=16), i == 0, i == 15, "g_pm")
+    cp("v", A("pint"), A("ps3", 0, 32))
+    ts(A("xao"), A("pint"), 2047, OPS.bitwise_and)
+    ts(A("xbo"), A("pint"), 11, OPS.arith_shift_right)
+    cp("v", A("xpb", 1, 33), A("xbo"))
+    slots(A("xao"), 32, ("u1", "u2", "u3", "u4", "u5"), A("xaou"))
+    runs("xpb", "ps5", "b", "offb", "exb")
+    mm(A("ps4"), A("mbb"), A("exb"), True, True, "g_mb")
+    cp("s", A("mb"), A("ps4"))
+    for h in range(8):
+        scaled(A("repf", 128 * h, 128 * h + 128), A("i16", 0, 128), A("mk", h, h + 1), "g_repf")
+
+    def to_natural(land, q, pa, pb):
+        mm(A(pa, 0, 128), A(land, 0, 256, step=2), A("ident"), True, True, "g_n0" + land)
+        mm(A(pb, 0, 128), A(land, 1, 256, step=2), A("ident"), True, True, "g_n1" + land)
+        cp("s", A(q, 0, 128), A(pa, 0, 128))
+        cp("v", A(q, 128, 256), A(pb, 0, 128))
+
+    arrival("land3", 32, "arr3")
+    to_natural("land3", "q3", "ps6", "ps7")
+    cp("v", ind(A("w2"), A("lau")), A("q3"))
+    for k in range(4):
+        mm(A("ps%d" % k), A("i16", 0, 128), A("w2", 512 * k, 512 * k + 512), True, True, "g_y%d" % k)
+        tt(A("yat", 512 * k, 512 * k + 512), A("ps%d" % k), A("far", 512 * k, 512 * k + 512), OPS.mult)
+    cp("v", A("s5", 0, 128), ind(A("yat"), A("lta", 0, 8)))
+    cp("s", A("s5", 128, 256), ind(A("yat"), A("lta", 8, 16)))
+
+    def at5(q):
+        return T["land5"][:, 32 * q:32 * q + 32]
+
+    send(far, "s5", 32, at5, "arr5")
+    send(near + sib, "s5", 32, at5, "arr5")
+    dma("y", ext(T["ya"][:, :], "ya"), A("yat", 0, 2048, 0, 16), "d_ya")
+    cp("s", A("land5", 32 * me, 32 * me + 32), A("s5", 224, 256))
+    fill(A("w3", 0, 2048), 0.0)
+    scaled(A("w4"), A("tf", 0, 2048), 0.0)
+
+    arrival("land5", 32, "arr5")
+    where5 = [(4, 0), (4, 1), (5, 0), (5, 1), (6, 0), (6, 1), (7, 0), (3, 0)]
+    for h in range(8):
+        k, c = where5[h]
+        mm(A("ps%d" % k, 256 * c, 256 * c + 256), A("repf", 128 * h, 128 * h + 128), A("land5"), True, True, "g_u%d" % k)
+    for q, k, h, n in (("v", 4, 0, 512), ("s", 5, 2, 512), ("v", 6, 4, 512), ("s", 7, 6, 256), ("v", 3, 7, 256)):
+        cp(q, A("ta", 256 * h, 256 * h + n), A("ps%d" % k, 0, n))
+    tt(A("wb"), ind(A("ta"), A("xaou")), A("vcp"), OPS.mult)
+    record("v", lambda: g.vector.tensor_tensor_scan(T["rb"][:, :], T["mb"][:, :], T["wb"][:, :], 0.0, OPS.mult, OPS.add),
+           [A("rb")], [A("mb"), A("wb")])
+    cp("v", ind(A("w3"), A("offb")), A("rb"))
+
+    add_slabs("w3", "s6", "land6", "arr6")
+    arrival("land6", 32, "arr6")
+    to_natural("land6", "q6", "ps2", "ps3")
+    cp("v", ind(A("w4"), A("lbu")), A("q6"))
+    for k in range(4):
+        n = "ps%d" % (4 + k)
+        mm((T[n][0:16, 0:512], A(n)[1]), A("i16", 0, 16), A("w4", 512 * k, 512 * k + 512), True, True, "g_z%d" % k)
+        cp("vs"[k % 2], A("ybt", 512 * k, 512 * k + 512, 0, 16), (T[n][0:16, 0:512], A(n)[1]))
+        dma("y", ext(T["yb"][:, 512 * k:512 * k + 512], "yb%d" % k), A("ybt", 512 * k, 512 * k + 512, 0, 16), "d_yb")
+    record("y", None, [], [(None, [("ext_ya", 0, 128, 0, 1)] + [("ext_yb%d" % k, 0, 128, 0, 1) for k in range(4)])])
+
+    bits = [0] * len(ops)
+    known = {}
+    need = set()
+    for k, o in enumerate(ops):
+        have = known.get(o["q"], 0)
+        waits = []
+        for j in sorted(o["dep"], reverse=True):
+            if have >> j & 1:
+                continue
+            members = groups[ops[j]["grp"]] if ops[j]["grp"] is not None else [j]
+            if k in members:
+                continue
+            assert max(members) < k
+            for m in members:
+                have |= bits[m]
+            waits.append(j)
+            need.add(j)
+        known[o["q"]] = have
+        bits[k] = have | 1 << k
+        o["waits"] = waits
+        o["have"] = have
+    needed_groups = set(ops[j]["grp"] for j in need if ops[j]["grp"] is not None)
+    chains, used, place, group_sem = [], [0], {}, {}
+
+    def fresh():
+        used[0] += 1
+        return "e%d" % (used[0] - 1)
+
+    for k, o in enumerate(ops):
+        if o["fixed"] is not None:
+            place[k] = o["fixed"]
+        elif o["grp"] in needed_groups and o["grp"] is not None:
+            if o["grp"] not in group_sem:
+                group_sem[o["grp"]] = fresh()
+            place[k] = (group_sem[o["grp"]], sum(ops[m]["inc"] for m in groups[o["grp"]]))
+        elif k in need:
+            for c in chains:
+                if c["q"] == o["q"] and o["have"] >> c["last"] & 1:
+                    break
+            else:
+                c = {"q": o["q"], "sem": fresh(), "last": None, "n": 0}
+                chains.append(c)
+            c["last"] = k
+            c["n"] += o["inc"]
+            place[k] = (c["sem"], c["n"])
+    assert used[0] <= NSEM, used[0]
+
+    for k, o in enumerate(ops):
+        if o["fixed"] is not None:
+            continue
+        q = queues[o["q"]]
+        best = {}
+        for j in o["waits"]:
+            s, v = place[j]
+            best[s] = max(v, best.get(s, 0))
+        for s in sorted(best):
+            q.wait_ge(T.sem[s], best[s])
+        if o["f"] is None:
+            continue
+        x = o["f"]()
+        if k in place:
+            x.then_inc(T.sem[place[k][0]], o["inc"])
+    g.wait_ge(T.sem["sent"], sent[0])

@@ -10,16 +10,17 @@ NDUMP = 640
 SCRATCH = {}
 for _n, _c, _t in [
         ("i1", 128, I32), ("i1b", 128, I32), ("i2", 8, I32), ("i2b", 8, I32), ("i3", 128, I32), ("i4", 128, I32),
-        ("i4b", 128, I32), ("i5", 128, I32), ("ki", 32, I32), ("kk", 32, U16), ("dj", 32, F),
-        ("mk", 8, F), ("i16", 512, F), ("z", 240, F), ("ident", 128, F), ("mbf", 128, F), ("mbb", 128, BFT),
+        ("i4b", 128, I32), ("i5", 128, I32), ("i6", 128, I32), ("i6b", 128, I32), ("i7", 8, I32), ("i7b", 8, I32),
+        ("ki", 32, I32), ("kk", 32, U16), ("dj", 32, F), ("o8", 128, F), ("mk8", 8, F), ("repc", 1024, BFT),
+        ("mk", 8, F), ("i16", 512, F), ("z", 144, F), ("ident", 128, F), ("mbf", 128, F), ("mbb", 128, BFT),
         ("e8", 128, F), ("rm", 4, F), ("n1", 128, F), ("n2", 128, F), ("p1", 128, F), ("p2", 128, F),
-        ("repb", 1024, BFT), ("repf", 1024, F),
+        ("repb", 1024, BFT), ("repf", 1024, F), ("cb", 256, BFT),
         ("tf", 4096, BFT), ("far", 2048, BFT), ("v8", 512, F), ("v16", 512, F), ("xi", 128, I32), ("ln", 32, I32),
         ("lau", 16, U16), ("lbu", 16, U16), ("lu", 32, U16), ("lta", 16, U16),
         ("t1", 64, I32), ("t2", 64, I32), ("t3", 64, I32), ("t4", 64, I32), ("t5", 64, I32), ("xu", 64, U16),
         ("obu", 32, U16), ("xpa", 34, F), ("xpb", 34, F),
         ("ea", 32, F), ("ca", 32, F), ("da", 32, F), ("fma", 32, F), ("ga", 32, F), ("offa", 32, U16),
-        ("eb", 32, F), ("cb", 32, F), ("db", 32, F), ("fmb", 32, F), ("gb", 32, F), ("offb", 32, U16),
+        ("eb", 32, F), ("cb2", 32, F), ("db", 32, F), ("fmb", 32, F), ("gb", 32, F), ("offb", 32, U16),
         ("exa", 512, BFT), ("exb", 512, BFT), ("ma", 512, F), ("mb", 512, F),
         ("pk0", 32, F), ("pk", 32, F), ("exp", 512, F), ("fp", 512, F), ("pm", 512, F), ("pint", 32, I32),
         ("xao", 32, I32), ("xbo", 32, I32), ("u1", 32, I32), ("u2", 32, I32), ("u3", 32, I32), ("u4", 32, I32),
@@ -27,7 +28,8 @@ for _n, _c, _t in [
         ("s1", 512, BFT), ("tb", 2048, BFT), ("tc", 2048, BFT), ("vc", 512, F), ("vcp", 512, F), ("wa", 512, F),
         ("ra", 512, F), ("w1", 2048 + NDUMP, F), ("s3", 256, F), ("q3", 256, F), ("w2", 2048, F), ("yat", 2048, F),
         ("s5", 256, F), ("land3", 256, F), ("land5", 256, F), ("land6", 256, F), ("ta", 2048, F), ("wb", 512, F),
-        ("rb", 512, F), ("w3", 2048 + NDUMP, F), ("s6", 256, F), ("q6", 256, F), ("w4", 2048, F), ("ybt", 2048, F)]:
+        ("rb", 512, F), ("w3", 2048 + NDUMP, F), ("s6", 256, F), ("q6", 256, F), ("w4", 2048, F), ("y1", 256, F),
+        ("y2", 256, F)]:
     SCRATCH[_n] = ("sbuf", [128, _c], _t)
 SCRATCH["ll"] = ("sbuf", [128, 3, 8, 2], I32)
 SCRATCH["llf"] = ("sbuf", [128, 8, 4], F)
@@ -37,8 +39,8 @@ SCRATCH["rra"] = ("sbuf", [128, 8, 8, 2], F)
 SCRATCH["land1"] = ("sbuf", [128, 16, 32], BFT)
 for _k in range(8):
     SCRATCH["ps%d" % _k] = ("psum", [128, 512], F)
-NSEM = 140
-SEMAPHORES = ["e%d" % k for k in range(NSEM)] + ["arr1", "arr3", "arr5", "arr6", "sent"]
+NSEM = 130
+SEMAPHORES = ["e%d" % k for k in range(NSEM)] + ["arr%d%s" % (k, s) for k in (1, 3, 5, 6) for s in "fn"] + ["sent"]
 
 
 def rank_program(g, core, T, topo):
@@ -97,10 +99,7 @@ def rank_program(g, core, T, topo):
             record(q, lambda: g.scalar.activation(out[0], in_[0], COPY), [out], [in_], grp)
 
     def scaled(out, in_, s, grp=None):
-        if isinstance(s, tuple):
-            record("s", lambda: g.scalar.activation(out[0], in_[0], COPY, scale=s[0]), [out], [in_, s], grp)
-        else:
-            record("s", lambda: g.scalar.activation(out[0], in_[0], COPY, scale=s), [out], [in_], grp)
+        record("s", lambda: g.scalar.activation(out[0], in_[0], COPY, scale=s[0]), [out], [in_, s], grp)
 
     def tt(out, a, b, o, grp=None):
         record("v", lambda: g.vector.tensor_tensor(out[0], a[0], b[0], o), [out], [a, b], grp)
@@ -127,17 +126,26 @@ def rank_program(g, core, T, topo):
         else:
             record("g", lambda: g.iota(out[0], pattern, base, cm), [out], [])
 
-    def dma(q, out, in_, grp):
+    def scan(out, keep, x):
+        record("v", lambda: g.vector.tensor_tensor_scan(out[0], keep[0], x[0], 0.0, OPS.mult, OPS.add), [out], [keep, x])
+
+    def dma(q, out, in_, grp, after=()):
         e = queues[q]
-        record(q, lambda: e.dma_start(out[0], in_[0]), [out], [in_], grp, 16)
+        record(q, lambda: e.dma_start(out[0], in_[0]), [out], [in_] + list(after), grp, 16)
 
     def ext(ap, n):
         return (ap, [("ext_" + n, 0, 128, 0, 1)])
 
-    sib = [q for q in range(len(cores)) if q != me and topo.chip(cores[q]) == here]
-    near = [q for q in range(len(cores)) if topo.same_plane(topo.chip(cores[q]), here)]
-    far = [q for q in range(len(cores)) if q != me and q not in sib and q not in near]
+    ranks = range(len(cores))
+    sib = [q for q in ranks if q != me and topo.chip(cores[q]) == here]
+    near = [q for q in ranks if topo.same_plane(topo.chip(cores[q]), here)]
+    far = [q for q in ranks if q != me and q not in sib and q not in near]
     order = far + near + sib + [me]
+
+    def pairs(qs):
+        return sorted(q for q in qs if q + 1 in qs and topo.chip(cores[q]) == topo.chip(cores[q + 1]))
+
+    waves = [pairs(far), pairs(near + sib + [me])]
 
     def share(q, dests, engines):
         n = len(engines) // len(dests)
@@ -154,40 +162,41 @@ def rank_program(g, core, T, topo):
             return share(q, near, off_chip)
         return on_chip[:len(on_chip) // 2]
 
-    n_in = sum(len(engines_for(q)) for q in far + near + sib)
     sent = [0]
 
-    def send(dests, src, width, dst, arr):
-        tr, rd = [], []
-        for q in dests:
-            d = order.index(q)
-            s = A(src, d * width, (d + 1) * width)
-            rd.append(s)
-            rid, pid = topo.addr(cores[q])[:2]
-            es = engines_for(q)
-            sent[0] += len(es)
-            tr.append(RemoteDMATransfer(dst_ids=[DstId(rid=rid, pnc=pid)], dma_engine_mask=sum(1 << e for e in es),
-                                        remote_sem=T.sem[arr], srcs=[s[0]], dsts=[dst(me)]))
-        record("g", lambda: g.remote_dma_fused(tr, local_sem=T.sem["sent"]), [], rd)
+    def send(src, width, dst, arr):
+        for dests, w in ((far, "f"), (near + sib, "n")):
+            tr, rd = [], []
+            for q in dests:
+                d = order.index(q)
+                s = A(src, d * width, (d + 1) * width)
+                rd.append(s)
+                rid, pid = topo.addr(cores[q])[:2]
+                es = engines_for(q)
+                sent[0] += len(es)
+                tr.append(RemoteDMATransfer(dst_ids=[DstId(rid=rid, pnc=pid)], dma_engine_mask=sum(1 << e for e in es),
+                                            remote_sem=T.sem[arr + w], srcs=[s[0]], dsts=[dst(me)]))
+            record("g", lambda tr=tr: g.remote_dma_fused(tr, local_sem=T.sem["sent"]), [], rd)
 
     def arrival(n, width, arr):
-        regs = [(n, 0, 128, q * width, (q + 1) * width) for q in range(len(cores)) if q != me]
-        record("in_" + arr, None, [(None, regs)], [], fixed=(arr, n_in))
+        for srcs, w in ((far, "f"), (near + sib, "n")):
+            regs = [(n, 0, 128, q * width, (q + 1) * width) for q in srcs]
+            record("in_" + arr + w, None, [(None, regs)], [], fixed=(arr + w, sum(len(engines_for(q)) for q in srcs)))
 
     dma("y", X(T["ll"][:, 0, :, :], "ll", 0, 16), ext(T["lb"][:, :], "lb"), "d_l")
     dma("y", X(T["ll"][:, 1, :, :], "ll", 16, 32), ext(T["lc"][:, :], "lc"), "d_l")
+    dma("s", A("cb"), ext(T["fc"][:, :], "fc"), "d_cb")
     for k in range(8):
-        dma("y", A("tf", 0, 2048, 16 * k, 16 * k + 16), ext(T["fb"][:, :], "fb"), "d_tf")
-        dma("s", A("tf", 2048, 4096, 16 * k, 16 * k + 16), ext(T["fc"][:, :], "fc"), "d_tf")
+        dma("ys"[k % 2], A("tf", 0, 2048, 16 * k, 16 * k + 16), ext(T["fb"][:, :], "fb"), "d_tf")
     for k, n in enumerate(("xa", "xb", "xc", "ob")):
         dma("y", A("xi", 32 * k, 32 * k + 32), ext(T[n][:, :], n), "d_x")
     dma("y", A("v8", 0, 512, 0, 8), ext(T["v"][:, :], "v"), "d_x")
     dma("y", X(T["ll"][:, 2, :, :], "ll", 32, 48), ext(T["la"][:, :], "la"), "d_x")
     dma("y", A("ln", 0, 16), ext(T["la"][:, :], "la"), "d_x")
     dma("y", A("ln", 16, 32), ext(T["lb"][:, :], "lb"), "d_x")
-    for k in range(8):
-        dma("y", A("far", 0, 2048, 16 * k, 16 * k + 16), ext(T["fa"][:, :], "fa"), "d_fa")
 
+    iota("i6", 128, [[0, 8], [-8, 16]], 0, 1)
+    iota("i7", 8, [[-1, 8]], 8, 1)
     iota("i2", 8, [[-16, 8]], 0, 1)
     iota("i1", 128, [[0, 8], [-1, 16]], 16, 1)
     iota("ki", 32, [[1, 32]], 0, 0)
@@ -196,23 +205,42 @@ def rank_program(g, core, T, topo):
     iota("i5", 128, [[1, 8], [0, 16]], 0, -1)
     iota("dj", 32, [[16, 32]], 2048, 1, True)
     fill(A("z"), 0.0)
-    fill(A("xpa"), -1.0)
-    fill(A("xpb"), -1.0)
+    ts(A("i6b"), A("i6"), 3, OPS.arith_shift_right)
+    ts(A("o8"), A("i6b"), 0, OPS.is_equal)
+    ts(A("i7b"), A("i7"), 7, OPS.bitwise_and)
+    ts(A("mk8"), A("i7b"), 0, OPS.is_equal)
     ts(A("i2b"), A("i2"), 4, OPS.arith_shift_right)
     ts(A("mk"), A("i2b"), 0, OPS.is_equal)
     ts(A("i1b"), A("i1"), 15, OPS.bitwise_and)
     ts(A("i16", 0, 128), A("i1b"), 0, OPS.is_equal)
     cp("v", A("z", 112, 128), A("i16", 0, 16))
+    fill(A("xpa"), -1.0)
+    fill(A("xpb"), -1.0)
+    cp("v", A("kk"), A("ki"))
+    for h in range(8):
+        scaled(A("repc", 128 * h, 128 * h + 128), A("o8"), A("mk8", h, h + 1), "g_repc")
 
+    for h in range(8):
+        mm(A("ps%d" % (h // 2), 256 * (h % 2), 256 * (h % 2) + 256), A("repc", 128 * h, 128 * h + 128), A("cb"),
+           True, True, "g_c%d" % (h // 2))
     ll, llf, rr = T["ll"], T["llf"], T["rr"]
     cp("v", X(llf[:, :, 0:2], "llf", 0, 1), X(ll[:, 0, :, :], "ll", 0, 16))
     ts(X(llf[:, :, 2:4], "llf", 1, 2), X(ll[:, 1, :, :], "ll", 16, 32), 2048, OPS.add)
     for d in range(8):
         r = order[d]
         ts(X(rr[:, :, d, :], "rr", d, d + 1), X(llf[:, :, :], "llf", 0, 2), A("mk", r, r + 1), OPS.mult, grp="g_rr")
-    for h in range(8):
-        mm(A("ps0", 0, 32), A("z", 112 - 16 * h, 240 - 16 * h), X(rr[:, h, :, :], "rr", 0, 8), h == 0, h == 7, "g_lt")
-    cp("v", A("lu"), A("ps0", 0, 32))
+
+    def to_blocked(ps, n, src, grp):
+        for h in range(8):
+            b = 32 * (h // 2)
+            mm((T[ps][b:b + 32, 0:n], [(ps, b, b + 32, 0, n)]), A("z", 112 - 16 * (h % 2), 144 - 16 * (h % 2)),
+               X(T[src][:, h, :, :], src, 0, 8), h % 2 == 0, h % 2 == 1, grp)
+
+    to_blocked("ps4", 32, "rr", "g_lt")
+    for k in range(3):
+        cp("s", A("tf", 2048 + 512 * k, 2560 + 512 * k), A("ps%d" % k))
+    cp("v", A("tf", 3584, 4096), A("ps3"))
+    cp("v", A("lu"), A("ps4", 0, 32))
     cp("v", A("s1", 0, 256), ind(A("tf"), A("lu", 0, 16)))
     cp("s", A("s1", 256, 512), ind(A("tf"), A("lu", 16, 32)))
 
@@ -221,8 +249,9 @@ def rank_program(g, core, T, topo):
     def at1(q):
         return land1[:, 2 * q:2 * q + 2, :]
 
-    send(far, "s1", 64, at1, "arr1")
-    send(near + sib, "s1", 64, at1, "arr1")
+    send("s1", 64, at1, "arr1")
+    iota("w1", 2048, [[0, 2048]], 0, 0, True)
+    iota("w2", 2048, [[0, 2048]], 0, 0, True)
     for f in range(2):
         cp("s", X(land1[:, 2 * me + f, :], "land1", 2 * me + f, 2 * me + f + 1),
            A("s1", 448 + 32 * f, 480 + 32 * f), "g_own1")
@@ -231,14 +260,6 @@ def rank_program(g, core, T, topo):
         scaled(A("repb", 128 * h, 128 * h + 128), A("i16", 0, 128), A("mk", h, h + 1), "g_repb")
     for k in range(1, 4):
         cp("s", A("i16", 128 * k, 128 * k + 128), A("i16", 0, 128), "g_i16")
-    cp("v", A("kk"), A("ki"))
-    ts(A("i4b"), A("i4"), 4, OPS.arith_shift_right)
-    ts(A("mbb"), A("i4b"), 0, OPS.is_equal)
-    ts(A("mbf"), A("i4b"), 0, OPS.is_equal)
-    ts(A("e8"), A("i5"), 0, OPS.is_equal)
-    mm(A("ps1"), A("e8", 0, 128, 0, 8), A("v8", 0, 512, 0, 8), True, True, "g_v")
-    cp("s", A("v16"), A("ps1"))
-
     cp("v", A("rm", 0, 1), A("i16", 0, 1))
     cp("v", A("rm", 1, 2), A("i16", 15, 16))
     ts(A("rm", 2, 3), A("i16", 0, 1), -1.0, OPS.mult, 1.0, OPS.add)
@@ -248,16 +269,21 @@ def rank_program(g, core, T, topo):
     ts(A("n2"), A("i3"), -15, OPS.is_equal, A("rm", 0, 1), OPS.mult, grp="g_sh")
     ts(A("p1"), A("i3"), -1, OPS.is_equal, A("rm", 3, 4), OPS.mult, grp="g_sh")
     ts(A("p2"), A("i3"), 15, OPS.is_equal, A("rm", 1, 2), OPS.mult, grp="g_sh")
+    ts(A("e8"), A("i5"), 0, OPS.is_equal)
+    mm(A("ps5"), A("e8", 0, 128, 0, 8), A("v8", 0, 512, 0, 8), True, True, "g_v")
+    cp("s", A("v16"), A("ps5"))
+    ts(A("i4b"), A("i4"), 4, OPS.arith_shift_right)
+    ts(A("mbb"), A("i4b"), 0, OPS.is_equal)
 
-    def runs(xp, ps, s, off, ex):
+    def runs(xp, ps, s, off, ex, c):
         mm(A(ps, 0, 32), A("n1"), A(xp, 1, 33), True, False, "g_n" + s)
         mm(A(ps, 0, 32), A("n2"), A(xp, 2, 34), False, True, "g_n" + s)
         mm(A(ps, 32, 64), A("p1"), A(xp, 1, 33), True, False, "g_n" + s)
         mm(A(ps, 32, 64), A("p2"), A(xp, 0, 32), False, True, "g_n" + s)
         tt(A("d" + s), A(xp, 1, 33), A("dj"), OPS.subtract)
-        tt(A("c" + s), A(ps, 32, 64), A(xp, 1, 33), OPS.is_equal)
+        tt(A(c), A(ps, 32, 64), A(xp, 1, 33), OPS.is_equal)
         tt(A("e" + s), A(ps, 0, 32), A(xp, 1, 33), OPS.not_equal)
-        tt(A(ex), ind(A("c" + s), A("kk")), A("i16"), OPS.mult)
+        tt(A(ex), ind(A(c), A("kk")), A("i16"), OPS.mult)
         tt(A("fm" + s), A("d" + s), A("e" + s), OPS.mult)
         tt(A("g" + s), A("fm" + s), A("dj"), OPS.add)
         cp("v", A(off), A("g" + s))
@@ -270,19 +296,35 @@ def rank_program(g, core, T, topo):
         tt(A(t[4], 0, n), A(t[3], 0, n), x, OPS.add)
         cp("v", out, A(t[4], 0, n))
 
-    runs("xpa", "ps7", "a", "offa", "exa")
+    runs("xpa", "ps7", "a", "offa", "exa", "ca")
     mm(A("ps6"), A("mbb"), A("exa"), True, True, "g_ma")
     cp("s", A("ma"), A("ps6"))
     slots(A("xi", 32, 96), 64, ("t1", "t2", "t3", "t4", "t5"), A("xu"))
-    fill(A("w1", 0, 2048), 0.0)
-    scaled(A("w2"), A("tf", 0, 2048), 0.0)
-    ts(A("ident"), A("i3"), 0, OPS.is_equal)
+    cp("v", A("obu"), A("xi", 96, 128))
+    laf = T["laf"]
+    cp("v", X(laf[:, :, :], "laf", 0, 1), X(ll[:, 2, :, :], "ll", 32, 48))
+    for d in range(8):
+        r = order[d]
+        scaled(X(T["rra"][:, :, d, :], "rra", d, d + 1), X(laf[:, :, :], "laf", 0, 1), A("mk", r, r + 1), grp="g_rra")
+    to_blocked("ps4", 16, "rra", "g_lta")
+    ts(A("mbf"), A("i4b"), 0, OPS.is_equal)
+    ts(A("pk0"), A("xi", 32, 64), 2048, OPS.mult)
+    tt(A("pk"), A("pk0"), A("xpa", 1, 33), OPS.add)
+    tt(A("exp"), ind(A("pk"), A("kk")), A("i16"), OPS.mult)
+    cp("v", A("lta"), A("ps4", 0, 16))
 
     arrival("land1", 2, "arr1")
-    for f, first in ((1, 0), (0, 4)):
-        for h in range(8):
-            mm(A("ps%d" % (first + h // 2), 256 * (h % 2), 256 * (h % 2) + 256), A("repb", 128 * h, 128 * h + 128),
-               X(land1[:, f::2, :], "land1", 0, 16), True, True, "g_t%d%d" % (f, h // 2))
+    for k in range(8):
+        dma("y", A("far", 0, 2048, 16 * k, 16 * k + 16), ext(T["fa"][:, :], "fa"), "d_fa",
+            [X(None, "land1", 2 * q, 2 * q + 2) for q in near])
+    for w in waves:
+        for f, first in ((1, 0), (0, 4)):
+            for h in range(8):
+                for q in w:
+                    c = 256 * (h % 2) + 32 * q
+                    mm(A("ps%d" % (first + h // 2), c, c + 64), A("repb", 128 * h, 128 * h + 128),
+                       X(land1[:, 2 * q + f:2 * q + 4:2, :], "land1", 2 * q, 2 * q + 4), True, True,
+                       "g_t%d%d" % (f, h // 2))
     for k in range(4):
         cp("vs"[k % 2], A("tc", 512 * k, 512 * k + 512), A("ps%d" % k))
     for k in range(3):
@@ -290,9 +332,11 @@ def rank_program(g, core, T, topo):
     tt(A("vc"), ind(A("tc"), A("xu", 32, 64)), A("v16"), OPS.mult)
     cp("v", A("tb", 1536, 2048), A("ps7"))
     tt(A("wa"), ind(A("tb"), A("xu", 0, 32)), A("vc"), OPS.mult)
-    record("v", lambda: g.vector.tensor_tensor_scan(T["ra"][:, :], T["ma"][:, :], T["wa"][:, :], 0.0, OPS.mult, OPS.add),
-           [A("ra")], [A("ma"), A("wa")])
+    scan(A("ra"), A("ma"), A("wa"))
     cp("v", ind(A("w1"), A("offa")), A("ra"))
+    mm(A("ps2"), A("mbf"), A("exp"), True, True, "g_fp")
+    cp("s", A("fp"), A("ps2"))
+    cp("s", A("vcp"), ind(A("vc"), A("obu")))
 
     def add_slabs(w, s, land, arr):
         for d in range(8):
@@ -303,44 +347,19 @@ def rank_program(g, core, T, topo):
                    True, True, "g_%s%d" % (w, d // 4))
         cp("v", A(s, 0, 128), A("ps0", 0, 128))
         cp("s", A(s, 128, 256), A("ps1", 0, 128))
-
-        def at(q):
-            return T[land][:, 32 * q:32 * q + 32]
-
-        send(far, s, 32, at, arr)
-        send(near + sib, s, 32, at, arr)
+        send(s, 32, lambda q: T[land][:, 32 * q:32 * q + 32], arr)
         cp("s", A(land, 32 * me, 32 * me + 32), A(s, 224, 256))
 
     add_slabs("w1", "s3", "land3", "arr3")
+    iota("w3", 2048, [[0, 2048]], 0, 0, True)
+    iota("w4", 2048, [[0, 2048]], 0, 0, True)
 
+    ts(A("ident"), A("i3"), 0, OPS.is_equal)
+    tt(A("pm"), ind(A("fp"), A("obu")), A("i16"), OPS.mult)
     cp("v", A("lau"), A("ln", 0, 16))
     cp("v", A("lbu"), A("ln", 16, 32))
-    laf, rra = T["laf"], T["rra"]
-    cp("v", X(laf[:, :, :], "laf", 0, 1), X(ll[:, 2, :, :], "ll", 32, 48))
-    for d in range(8):
-        r = order[d]
-        ts(X(rra[:, :, d, :], "rra", d, d + 1), X(laf[:, :, :], "laf", 0, 1), A("mk", r, r + 1), OPS.mult, grp="g_rra")
-    for h in range(8):
-        mm(A("ps4", 0, 16), A("z", 112 - 16 * h, 240 - 16 * h), X(rra[:, h, :, :], "rra", 0, 8), h == 0, h == 7, "g_lta")
-    cp("v", A("obu"), A("xi", 96, 128))
-    ts(A("pk0"), A("xi", 32, 64), 2048, OPS.mult)
-    tt(A("pk"), A("pk0"), A("xpa", 1, 33), OPS.add)
-    tt(A("exp"), ind(A("pk"), A("kk")), A("i16"), OPS.mult)
-    cp("v", A("lta"), A("ps4", 0, 16))
-    mm(A("ps2"), A("mbf"), A("exp"), True, True, "g_fp")
-    cp("s", A("fp"), A("ps2"))
-    cp("s", A("vcp"), ind(A("vc"), A("obu")))
-    tt(A("pm"), ind(A("fp"), A("obu")), A("i16"), OPS.mult)
     for i in range(16):
         mm(A("ps3", 0, 32), A("ident"), A("pm", i, 512, step=16), i == 0, i == 15, "g_pm")
-    cp("v", A("pint"), A("ps3", 0, 32))
-    ts(A("xao"), A("pint"), 2047, OPS.bitwise_and)
-    ts(A("xbo"), A("pint"), 11, OPS.arith_shift_right)
-    cp("v", A("xpb", 1, 33), A("xbo"))
-    slots(A("xao"), 32, ("u1", "u2", "u3", "u4", "u5"), A("xaou"))
-    runs("xpb", "ps5", "b", "offb", "exb")
-    mm(A("ps4"), A("mbb"), A("exb"), True, True, "g_mb")
-    cp("s", A("mb"), A("ps4"))
     for h in range(8):
         scaled(A("repf", 128 * h, 128 * h + 128), A("i16", 0, 128), A("mk", h, h + 1), "g_repf")
 
@@ -353,44 +372,52 @@ def rank_program(g, core, T, topo):
     arrival("land3", 32, "arr3")
     to_natural("land3", "q3", "ps6", "ps7")
     cp("v", ind(A("w2"), A("lau")), A("q3"))
-    for k in range(4):
-        mm(A("ps%d" % k), A("i16", 0, 128), A("w2", 512 * k, 512 * k + 512), True, True, "g_y%d" % k)
-        tt(A("yat", 512 * k, 512 * k + 512), A("ps%d" % k), A("far", 512 * k, 512 * k + 512), OPS.mult)
+    for k, lo, n in ((0, 0, 512), (1, 512, 512), (2, 1024, 512), (5, 1536, 256), (4, 1792, 256)):
+        mm(A("ps%d" % k, 0, n), A("i16", 0, 128), A("w2", lo, lo + n), True, True, "g_y%d" % k)
+        tt(A("yat", lo, lo + n), A("ps%d" % k, 0, n), A("far", lo, lo + n), OPS.mult)
     cp("v", A("s5", 0, 128), ind(A("yat"), A("lta", 0, 8)))
     cp("s", A("s5", 128, 256), ind(A("yat"), A("lta", 8, 16)))
-
-    def at5(q):
-        return T["land5"][:, 32 * q:32 * q + 32]
-
-    send(far, "s5", 32, at5, "arr5")
-    send(near + sib, "s5", 32, at5, "arr5")
-    dma("y", ext(T["ya"][:, :], "ya"), A("yat", 0, 2048, 0, 16), "d_ya")
+    send("s5", 32, lambda q: T["land5"][:, 32 * q:32 * q + 32], "arr5")
     cp("s", A("land5", 32 * me, 32 * me + 32), A("s5", 224, 256))
-    fill(A("w3", 0, 2048), 0.0)
-    scaled(A("w4"), A("tf", 0, 2048), 0.0)
+
+    cp("v", A("pint"), A("ps3", 0, 32))
+    ts(A("xbo"), A("pint"), 11, OPS.arith_shift_right)
+    cp("v", A("xpb", 1, 33), A("xbo"))
+    runs("xpb", "ps1", "b", "offb", "exb", "cb2")
+    mm(A("ps2"), A("mbb"), A("exb"), True, True, "g_mb")
+    cp("s", A("mb"), A("ps2"))
+    ts(A("xao"), A("pint"), 2047, OPS.bitwise_and)
+    slots(A("xao"), 32, ("u1", "u2", "u3", "u4", "u5"), A("xaou"))
 
     arrival("land5", 32, "arr5")
+    dma("y", ext(T["ya"][:, :], "ya"), A("yat", 0, 2048, 0, 16), "d_ya",
+        [X(None, "land5", 32 * q, 32 * q + 32) for q in near])
     where5 = [(4, 0), (4, 1), (5, 0), (5, 1), (6, 0), (6, 1), (7, 0), (3, 0)]
-    for h in range(8):
-        k, c = where5[h]
-        mm(A("ps%d" % k, 256 * c, 256 * c + 256), A("repf", 128 * h, 128 * h + 128), A("land5"), True, True, "g_u%d" % k)
+    for w in waves:
+        for h in range(8):
+            for q in w:
+                k, c = where5[h][0], 256 * where5[h][1] + 32 * q
+                mm(A("ps%d" % k, c, c + 64), A("repf", 128 * h, 128 * h + 128), A("land5", 32 * q, 32 * q + 64),
+                   True, True, "g_u%d" % k)
     for q, k, h, n in (("v", 4, 0, 512), ("s", 5, 2, 512), ("v", 6, 4, 512), ("s", 7, 6, 256), ("v", 3, 7, 256)):
         cp(q, A("ta", 256 * h, 256 * h + n), A("ps%d" % k, 0, n))
     tt(A("wb"), ind(A("ta"), A("xaou")), A("vcp"), OPS.mult)
-    record("v", lambda: g.vector.tensor_tensor_scan(T["rb"][:, :], T["mb"][:, :], T["wb"][:, :], 0.0, OPS.mult, OPS.add),
-           [A("rb")], [A("mb"), A("wb")])
+    scan(A("rb"), A("mb"), A("wb"))
     cp("v", ind(A("w3"), A("offb")), A("rb"))
 
     add_slabs("w3", "s6", "land6", "arr6")
     arrival("land6", 32, "arr6")
     to_natural("land6", "q6", "ps2", "ps3")
     cp("v", ind(A("w4"), A("lbu")), A("q6"))
-    for k in range(4):
-        n = "ps%d" % (4 + k)
-        mm((T[n][0:16, 0:512], A(n)[1]), A("i16", 0, 16), A("w4", 512 * k, 512 * k + 512), True, True, "g_z%d" % k)
-        cp("vs"[k % 2], A("ybt", 512 * k, 512 * k + 512, 0, 16), (T[n][0:16, 0:512], A(n)[1]))
-        dma("y", ext(T["yb"][:, 512 * k:512 * k + 512], "yb%d" % k), A("ybt", 512 * k, 512 * k + 512, 0, 16), "d_yb")
-    record("y", None, [], [(None, [("ext_ya", 0, 128, 0, 1)] + [("ext_yb%d" % k, 0, 128, 0, 1) for k in range(4)])])
+    for k in range(16):
+        mm(A("ps%d" % (4 + k // 8), k % 8, 128, step=8), A("w4", 128 * k, 128 * k + 128), A("i16", 0, 16), True, True,
+           "g_z%d" % (k // 8))
+    for k in range(2):
+        cp("vs"[k], A("y1", 128 * k, 128 * k + 128), A("ps%d" % (4 + k), 0, 128))
+        mm(A("ps%d" % (6 + k), 0, 128), A("y1", 128 * k, 128 * k + 128), A("ident"), True, True, "g_b%d" % k)
+        cp("vs"[k], A("y2", 128 * k, 128 * k + 128), A("ps%d" % (6 + k), 0, 128))
+        dma("ys"[k], ext(T["yb"][:, 1024 * k:1024 * k + 1024], "yb%d" % k), A("y2", 128 * k, 128 * k + 128), "d_yb%d" % k)
+    record("y", None, [], [(None, [("ext_" + n, 0, 128, 0, 1) for n in ("ya", "yb0", "yb1")])])
 
     bits = [0] * len(ops)
     known = {}

@@ -9,22 +9,21 @@ F, BFT, I32, U16 = "float32", "bfloat16", "int32", "uint16"
 NDUMP = 640
 SCRATCH = {}
 for _n, _c, _t in [
-        ("i1", 128, I32), ("i1b", 128, I32), ("i2", 8, I32), ("i2b", 8, I32), ("i3", 128, I32), ("i4", 128, I32),
-        ("i4b", 128, I32), ("i5", 128, I32), ("i6", 128, I32), ("i6b", 128, I32), ("i7", 8, I32), ("i7b", 8, I32),
-        ("ki", 32, I32), ("kk", 32, U16), ("dj", 32, F), ("o8", 128, F), ("mk8", 8, F), ("repc", 1024, BFT),
+        ("i1", 128, I32), ("i1b", 128, I32), ("i2", 8, I32), ("i2b", 8, I32), ("i4", 128, I32),
+        ("i4b", 128, I32), ("i5", 128, I32), ("ki", 32, I32), ("kk", 32, U16), ("dj", 32, F),
         ("mk", 8, F), ("i16", 512, F), ("z", 144, F), ("ident", 128, F), ("mbf", 128, F), ("mbb", 128, BFT),
-        ("e8", 128, F), ("rm", 4, F), ("n1", 128, F), ("n2", 128, F), ("p1", 128, F), ("p2", 128, F),
+        ("e8", 128, F), ("n1", 128, F), ("n2", 128, F), ("p1", 128, F), ("p2", 128, F),
         ("repb", 1024, BFT), ("repf", 1024, F), ("cb", 256, BFT),
         ("tf", 4096, BFT), ("far", 2048, BFT), ("v8", 512, F), ("v16", 512, F), ("xi", 128, I32), ("ln", 32, I32),
-        ("lau", 16, U16), ("lbu", 16, U16), ("lu", 32, U16), ("lta", 16, U16),
-        ("t1", 64, I32), ("t2", 64, I32), ("t3", 64, I32), ("t4", 64, I32), ("t5", 64, I32), ("xu", 64, U16),
+        ("lau", 16, U16), ("lbu", 16, U16), ("lu", 32, U16), ("lta", 16, U16), ("t1", 64, I32), ("t2", 64, I32),
+        ("t3", 64, I32), ("t4", 64, I32), ("t5", 64, I32), ("t6", 64, I32), ("xu", 64, U16),
         ("obu", 32, U16), ("xpa", 34, F), ("xpb", 34, F),
         ("ea", 32, F), ("ca", 32, F), ("da", 32, F), ("fma", 32, F), ("ga", 32, F), ("offa", 32, U16),
         ("eb", 32, F), ("cb2", 32, F), ("db", 32, F), ("fmb", 32, F), ("gb", 32, F), ("offb", 32, U16),
         ("exa", 512, BFT), ("exb", 512, BFT), ("ma", 512, F), ("mb", 512, F),
         ("pk0", 32, F), ("pk", 32, F), ("exp", 512, F), ("fp", 512, F), ("pm", 512, F), ("pint", 32, I32),
         ("xao", 32, I32), ("xbo", 32, I32), ("u1", 32, I32), ("u2", 32, I32), ("u3", 32, I32), ("u4", 32, I32),
-        ("u5", 32, I32), ("xaou", 32, U16),
+        ("u5", 32, I32), ("u6", 32, I32), ("xaou", 32, U16),
         ("s1", 512, BFT), ("tb", 2048, BFT), ("tc", 2048, BFT), ("vc", 512, F), ("vcp", 512, F), ("wa", 512, F),
         ("ra", 512, F), ("w1", 2048 + NDUMP, F), ("s3", 256, F), ("q3", 256, F), ("w2", 2048, F), ("yat", 2048, F),
         ("s5", 256, F), ("land3", 256, F), ("land5", 256, F), ("land6", 256, F), ("ta", 2048, F), ("wb", 512, F),
@@ -40,7 +39,7 @@ SCRATCH["land1"] = ("sbuf", [128, 16, 32], BFT)
 for _k in range(8):
     SCRATCH["ps%d" % _k] = ("psum", [128, 512], F)
 NSEM = 130
-SEMAPHORES = ["e%d" % k for k in range(NSEM)] + ["arr%d%s" % (k, s) for k in (1, 3, 5, 6) for s in "fn"] + ["sent"]
+SEMAPHORES = ["e%d" % k for k in range(NSEM)] + ["arr%d%s" % (k, s) for k in (1, 3, 5, 6) for s in "fsn"] + ["sent"]
 
 
 def rank_program(g, core, T, topo):
@@ -126,6 +125,10 @@ def rank_program(g, core, T, topo):
         else:
             record("g", lambda: g.iota(out[0], pattern, base, cm), [out], [])
 
+    def pick(n, base):
+        out, same = A(n), A("mbf")
+        record("g", lambda: g.affine_select(out[0], same[0], [[-1, 128]], OPS.is_equal, 0.0, base, 1), [out], [same])
+
     def scan(out, keep, x):
         record("v", lambda: g.vector.tensor_tensor_scan(out[0], keep[0], x[0], 0.0, OPS.mult, OPS.add), [out], [keep, x])
 
@@ -145,7 +148,7 @@ def rank_program(g, core, T, topo):
     def pairs(qs):
         return sorted(q for q in qs if q + 1 in qs and topo.chip(cores[q]) == topo.chip(cores[q + 1]))
 
-    waves = [pairs(far), pairs(near + sib + [me])]
+    p_own, p_far, p_near = pairs(sib + [me])[0], pairs(far), pairs(near)[0]
 
     def share(q, dests, engines):
         n = len(engines) // len(dests)
@@ -164,8 +167,11 @@ def rank_program(g, core, T, topo):
 
     sent = [0]
 
-    def send(src, width, dst, arr):
-        for dests, w in ((far, "f"), (near + sib, "n")):
+    def kind(q):
+        return "f" if q in far else "n" if q in near else "s"
+
+    def send(src, width, dst, arr, early):
+        for dests in (far + sib, near) if early else (far, near + sib):
             tr, rd = [], []
             for q in dests:
                 d = order.index(q)
@@ -175,19 +181,20 @@ def rank_program(g, core, T, topo):
                 es = engines_for(q)
                 sent[0] += len(es)
                 tr.append(RemoteDMATransfer(dst_ids=[DstId(rid=rid, pnc=pid)], dma_engine_mask=sum(1 << e for e in es),
-                                            remote_sem=T.sem[arr + w], srcs=[s[0]], dsts=[dst(me)]))
+                                            remote_sem=T.sem[arr + kind(q)], srcs=[s[0]], dsts=[dst(me)]))
             record("g", lambda tr=tr: g.remote_dma_fused(tr, local_sem=T.sem["sent"]), [], rd)
 
     def arrival(n, width, arr):
-        for srcs, w in ((far, "f"), (near + sib, "n")):
+        for srcs, w in ((sib, "s"), (far, "f"), (near, "n")):
             regs = [(n, 0, 128, q * width, (q + 1) * width) for q in srcs]
             record("in_" + arr + w, None, [(None, regs)], [], fixed=(arr + w, sum(len(engines_for(q)) for q in srcs)))
 
     dma("y", X(T["ll"][:, 0, :, :], "ll", 0, 16), ext(T["lb"][:, :], "lb"), "d_l")
     dma("y", X(T["ll"][:, 1, :, :], "ll", 16, 32), ext(T["lc"][:, :], "lc"), "d_l")
-    dma("s", A("cb"), ext(T["fc"][:, :], "fc"), "d_cb")
+    for h in range(8):
+        dma("s", A("cb", 0, 256, 16 * h, 16 * h + 16), ext(T["fc"][:, 256 * h:256 * h + 256], "fc"), "d_cb")
     for k in range(8):
-        dma("ys"[k % 2], A("tf", 0, 2048, 16 * k, 16 * k + 16), ext(T["fb"][:, :], "fb"), "d_tf")
+        dma("s" if k > 5 else "y", A("tf", 0, 2048, 16 * k, 16 * k + 16), ext(T["fb"][:, :], "fb"), "d_tf")
     for k, n in enumerate(("xa", "xb", "xc", "ob")):
         dma("y", A("xi", 32 * k, 32 * k + 32), ext(T[n][:, :], n), "d_x")
     dma("y", A("v8", 0, 512, 0, 8), ext(T["v"][:, :], "v"), "d_x")
@@ -195,20 +202,13 @@ def rank_program(g, core, T, topo):
     dma("y", A("ln", 0, 16), ext(T["la"][:, :], "la"), "d_x")
     dma("y", A("ln", 16, 32), ext(T["lb"][:, :], "lb"), "d_x")
 
-    iota("i6", 128, [[0, 8], [-8, 16]], 0, 1)
-    iota("i7", 8, [[-1, 8]], 8, 1)
     iota("i2", 8, [[-16, 8]], 0, 1)
     iota("i1", 128, [[0, 8], [-1, 16]], 16, 1)
-    iota("ki", 32, [[1, 32]], 0, 0)
-    iota("i3", 128, [[-1, 128]], 0, 1)
     iota("i4", 128, [[-16, 8], [0, 16]], 0, 1)
+    iota("ki", 32, [[1, 32]], 0, 0)
     iota("i5", 128, [[1, 8], [0, 16]], 0, -1)
     iota("dj", 32, [[16, 32]], 2048, 1, True)
     fill(A("z"), 0.0)
-    ts(A("i6b"), A("i6"), 3, OPS.arith_shift_right)
-    ts(A("o8"), A("i6b"), 0, OPS.is_equal)
-    ts(A("i7b"), A("i7"), 7, OPS.bitwise_and)
-    ts(A("mk8"), A("i7b"), 0, OPS.is_equal)
     ts(A("i2b"), A("i2"), 4, OPS.arith_shift_right)
     ts(A("mk"), A("i2b"), 0, OPS.is_equal)
     ts(A("i1b"), A("i1"), 15, OPS.bitwise_and)
@@ -217,11 +217,15 @@ def rank_program(g, core, T, topo):
     fill(A("xpa"), -1.0)
     fill(A("xpb"), -1.0)
     cp("v", A("kk"), A("ki"))
+    ts(A("i4b"), A("i4"), 4, OPS.arith_shift_right)
+    ts(A("mbf"), A("i4b"), 0, OPS.is_equal)
+    for n, k in (("n1", -1), ("n2", 15), ("p1", 1), ("p2", -15)):
+        pick(n, k)
     for h in range(8):
-        scaled(A("repc", 128 * h, 128 * h + 128), A("o8"), A("mk8", h, h + 1), "g_repc")
+        scaled(A("repb", 128 * h, 128 * h + 128), A("i16", 0, 128), A("mk", h, h + 1), "g_repb")
 
     for h in range(8):
-        mm(A("ps%d" % (h // 2), 256 * (h % 2), 256 * (h % 2) + 256), A("repc", 128 * h, 128 * h + 128), A("cb"),
+        mm(A("ps%d" % (h // 2), 256 * (h % 2), 256 * (h % 2) + 256), A("repb", 128 * h, 128 * h + 128), A("cb"),
            True, True, "g_c%d" % (h // 2))
     ll, llf, rr = T["ll"], T["llf"], T["rr"]
     cp("v", X(llf[:, :, 0:2], "llf", 0, 1), X(ll[:, 0, :, :], "ll", 0, 16))
@@ -237,9 +241,8 @@ def rank_program(g, core, T, topo):
                X(T[src][:, h, :, :], src, 0, 8), h % 2 == 0, h % 2 == 1, grp)
 
     to_blocked("ps4", 32, "rr", "g_lt")
-    for k in range(3):
-        cp("s", A("tf", 2048 + 512 * k, 2560 + 512 * k), A("ps%d" % k))
-    cp("v", A("tf", 3584, 4096), A("ps3"))
+    for k in range(4):
+        cp("sssv"[k], A("tf", 2048 + 512 * k, 2560 + 512 * k), A("ps%d" % k))
     cp("v", A("lu"), A("ps4", 0, 32))
     cp("v", A("s1", 0, 256), ind(A("tf"), A("lu", 0, 16)))
     cp("s", A("s1", 256, 512), ind(A("tf"), A("lu", 16, 32)))
@@ -249,37 +252,27 @@ def rank_program(g, core, T, topo):
     def at1(q):
         return land1[:, 2 * q:2 * q + 2, :]
 
-    send("s1", 64, at1, "arr1")
+    send("s1", 64, at1, "arr1", True)
+    pick("ident", 0)
     iota("w1", 2048, [[0, 2048]], 0, 0, True)
     iota("w2", 2048, [[0, 2048]], 0, 0, True)
     for f in range(2):
         cp("s", X(land1[:, 2 * me + f, :], "land1", 2 * me + f, 2 * me + f + 1),
            A("s1", 448 + 32 * f, 480 + 32 * f), "g_own1")
 
-    for h in range(8):
-        scaled(A("repb", 128 * h, 128 * h + 128), A("i16", 0, 128), A("mk", h, h + 1), "g_repb")
     for k in range(1, 4):
         cp("s", A("i16", 128 * k, 128 * k + 128), A("i16", 0, 128), "g_i16")
-    cp("v", A("rm", 0, 1), A("i16", 0, 1))
-    cp("v", A("rm", 1, 2), A("i16", 15, 16))
-    ts(A("rm", 2, 3), A("i16", 0, 1), -1.0, OPS.mult, 1.0, OPS.add)
-    ts(A("rm", 3, 4), A("i16", 15, 16), -1.0, OPS.mult, 1.0, OPS.add)
     cp("v", A("xpa", 1, 33), A("xi", 0, 32))
-    ts(A("n1"), A("i3"), 1, OPS.is_equal, A("rm", 2, 3), OPS.mult, grp="g_sh")
-    ts(A("n2"), A("i3"), -15, OPS.is_equal, A("rm", 0, 1), OPS.mult, grp="g_sh")
-    ts(A("p1"), A("i3"), -1, OPS.is_equal, A("rm", 3, 4), OPS.mult, grp="g_sh")
-    ts(A("p2"), A("i3"), 15, OPS.is_equal, A("rm", 1, 2), OPS.mult, grp="g_sh")
     ts(A("e8"), A("i5"), 0, OPS.is_equal)
-    mm(A("ps5"), A("e8", 0, 128, 0, 8), A("v8", 0, 512, 0, 8), True, True, "g_v")
-    cp("s", A("v16"), A("ps5"))
-    ts(A("i4b"), A("i4"), 4, OPS.arith_shift_right)
-    ts(A("mbb"), A("i4b"), 0, OPS.is_equal)
+    ts(A("pk0"), A("xi", 32, 64), 2048, OPS.mult)
 
-    def runs(xp, ps, s, off, ex, c):
+    def shift(xp, ps, s):
         mm(A(ps, 0, 32), A("n1"), A(xp, 1, 33), True, False, "g_n" + s)
         mm(A(ps, 0, 32), A("n2"), A(xp, 2, 34), False, True, "g_n" + s)
         mm(A(ps, 32, 64), A("p1"), A(xp, 1, 33), True, False, "g_n" + s)
         mm(A(ps, 32, 64), A("p2"), A(xp, 0, 32), False, True, "g_n" + s)
+
+    def runs(xp, ps, s, off, ex, c):
         tt(A("d" + s), A(xp, 1, 33), A("dj"), OPS.subtract)
         tt(A(c), A(ps, 32, 64), A(xp, 1, 33), OPS.is_equal)
         tt(A("e" + s), A(ps, 0, 32), A(xp, 1, 33), OPS.not_equal)
@@ -290,50 +283,43 @@ def rank_program(g, core, T, topo):
 
     def slots(x, n, t, out):
         ts(A(t[0], 0, n), x, 5, OPS.arith_shift_right, 7, OPS.bitwise_and)
-        ts(A(t[1], 0, n), x, 8, OPS.arith_shift_right)
-        tt(A(t[2], 0, n), A(t[0], 0, n), A(t[1], 0, n), OPS.subtract)
-        ts(A(t[3], 0, n), A(t[2], 0, n), 224, OPS.mult)
-        tt(A(t[4], 0, n), A(t[3], 0, n), x, OPS.add)
-        cp("v", out, A(t[4], 0, n))
+        ts(A(t[1], 0, n), x, 8, OPS.arith_shift_right, 1, OPS.bitwise_and)
+        ts(A(t[2], 0, n), A(t[0], 0, n), 32, OPS.mult)
+        ts(A(t[3], 0, n), A(t[1], 0, n), -224, OPS.mult)
+        tt(A(t[4], 0, n), A(t[2], 0, n), x, OPS.add)
+        tt(A(t[5], 0, n), A(t[3], 0, n), A(t[4], 0, n), OPS.add)
+        cp("v", out, A(t[5], 0, n))
 
-    runs("xpa", "ps7", "a", "offa", "exa", "ca")
-    mm(A("ps6"), A("mbb"), A("exa"), True, True, "g_ma")
-    cp("s", A("ma"), A("ps6"))
-    slots(A("xi", 32, 96), 64, ("t1", "t2", "t3", "t4", "t5"), A("xu"))
+    shift("xpa", "ps7", "a")
+    mm(A("ps5"), A("e8", 0, 128, 0, 8), A("v8", 0, 512, 0, 8), True, True, "g_v")
+    tt(A("pk"), A("pk0"), A("xpa", 1, 33), OPS.add)
+    cp("s", A("v16"), A("ps5"))
+    cp("v", A("mbb"), A("mbf"))
+    slots(A("xi", 32, 96), 64, ("t1", "t2", "t3", "t4", "t5", "t6"), A("xu"))
     cp("v", A("obu"), A("xi", 96, 128))
     laf = T["laf"]
     cp("v", X(laf[:, :, :], "laf", 0, 1), X(ll[:, 2, :, :], "ll", 32, 48))
-    for d in range(8):
-        r = order[d]
-        scaled(X(T["rra"][:, :, d, :], "rra", d, d + 1), X(laf[:, :, :], "laf", 0, 1), A("mk", r, r + 1), grp="g_rra")
-    to_blocked("ps4", 16, "rra", "g_lta")
-    ts(A("mbf"), A("i4b"), 0, OPS.is_equal)
-    ts(A("pk0"), A("xi", 32, 64), 2048, OPS.mult)
-    tt(A("pk"), A("pk0"), A("xpa", 1, 33), OPS.add)
-    tt(A("exp"), ind(A("pk"), A("kk")), A("i16"), OPS.mult)
-    cp("v", A("lta"), A("ps4", 0, 16))
+    runs("xpa", "ps7", "a", "offa", "exa", "ca")
 
     arrival("land1", 2, "arr1")
     for k in range(8):
         dma("y", A("far", 0, 2048, 16 * k, 16 * k + 16), ext(T["fa"][:, :], "fa"), "d_fa",
             [X(None, "land1", 2 * q, 2 * q + 2) for q in near])
-    for w in waves:
-        for f, first in ((1, 0), (0, 4)):
-            for h in range(8):
-                for q in w:
-                    c = 256 * (h % 2) + 32 * q
-                    mm(A("ps%d" % (first + h // 2), c, c + 64), A("repb", 128 * h, 128 * h + 128),
-                       X(land1[:, 2 * q + f:2 * q + 4:2, :], "land1", 2 * q, 2 * q + 4), True, True,
-                       "g_t%d%d" % (f, h // 2))
-    for k in range(4):
-        cp("vs"[k % 2], A("tc", 512 * k, 512 * k + 512), A("ps%d" % k))
-    for k in range(3):
-        cp("s", A("tb", 512 * k, 512 * k + 512), A("ps%d" % (4 + k)))
+    for f, q, k, h0, h1, e in ((1, p_own, 0, 0, 8, "v"), (0, p_own, 4, 0, 8, "s"), (1, p_far[0], 1, 0, 8, "v"),
+                               (1, p_far[1], 2, 0, 8, "s"), (0, p_far[0], 5, 0, 8, "v"), (0, p_far[1], 6, 0, 8, "s"),
+                               (1, p_near, 3, 0, 4, "v"), (1, p_near, 0, 4, 8, "s"), (0, p_near, 7, 0, 8, "s")):
+        for h in range(h0, h1):
+            mm(A("ps%d" % k, 64 * (h - h0), 64 * (h - h0) + 64), A("repb", 128 * h, 128 * h + 128),
+               X(land1[:, 2 * q + f:2 * q + 4:2, :], "land1", 2 * q, 2 * q + 4), True, True, "g_t%d%d" % (k, h0))
+        cp(e, A("tb" if f == 0 else "tc", 256 * q + 64 * h0, 256 * q + 64 * h1), A("ps%d" % k, 0, 64 * (h1 - h0)))
+    mm(A("ps1"), A("mbb"), A("exa"), True, True, "g_ma")
+    cp("s", A("ma"), A("ps1"))
     tt(A("vc"), ind(A("tc"), A("xu", 32, 64)), A("v16"), OPS.mult)
-    cp("v", A("tb", 1536, 2048), A("ps7"))
     tt(A("wa"), ind(A("tb"), A("xu", 0, 32)), A("vc"), OPS.mult)
     scan(A("ra"), A("ma"), A("wa"))
     cp("v", ind(A("w1"), A("offa")), A("ra"))
+    for i in range(16):
+        scaled(A("exp", i, 512, step=16), A("pk"), A("i16", i, i + 1), "g_exp")
     mm(A("ps2"), A("mbf"), A("exp"), True, True, "g_fp")
     cp("s", A("fp"), A("ps2"))
     cp("s", A("vcp"), ind(A("vc"), A("obu")))
@@ -347,17 +333,21 @@ def rank_program(g, core, T, topo):
                    True, True, "g_%s%d" % (w, d // 4))
         cp("v", A(s, 0, 128), A("ps0", 0, 128))
         cp("s", A(s, 128, 256), A("ps1", 0, 128))
-        send(s, 32, lambda q: T[land][:, 32 * q:32 * q + 32], arr)
+        send(s, 32, lambda q: T[land][:, 32 * q:32 * q + 32], arr, False)
         cp("s", A(land, 32 * me, 32 * me + 32), A(s, 224, 256))
 
     add_slabs("w1", "s3", "land3", "arr3")
     iota("w3", 2048, [[0, 2048]], 0, 0, True)
     iota("w4", 2048, [[0, 2048]], 0, 0, True)
 
-    ts(A("ident"), A("i3"), 0, OPS.is_equal)
     tt(A("pm"), ind(A("fp"), A("obu")), A("i16"), OPS.mult)
     cp("v", A("lau"), A("ln", 0, 16))
     cp("v", A("lbu"), A("ln", 16, 32))
+    for d in range(8):
+        r = order[d]
+        scaled(X(T["rra"][:, :, d, :], "rra", d, d + 1), X(laf[:, :, :], "laf", 0, 1), A("mk", r, r + 1), grp="g_rra")
+    to_blocked("ps4", 16, "rra", "g_lta")
+    cp("v", A("lta"), A("ps4", 0, 16))
     for i in range(16):
         mm(A("ps3", 0, 32), A("ident"), A("pm", i, 512, step=16), i == 0, i == 15, "g_pm")
     for h in range(8):
@@ -377,30 +367,28 @@ def rank_program(g, core, T, topo):
         tt(A("yat", lo, lo + n), A("ps%d" % k, 0, n), A("far", lo, lo + n), OPS.mult)
     cp("v", A("s5", 0, 128), ind(A("yat"), A("lta", 0, 8)))
     cp("s", A("s5", 128, 256), ind(A("yat"), A("lta", 8, 16)))
-    send("s5", 32, lambda q: T["land5"][:, 32 * q:32 * q + 32], "arr5")
+    send("s5", 32, lambda q: T["land5"][:, 32 * q:32 * q + 32], "arr5", True)
     cp("s", A("land5", 32 * me, 32 * me + 32), A("s5", 224, 256))
 
     cp("v", A("pint"), A("ps3", 0, 32))
     ts(A("xbo"), A("pint"), 11, OPS.arith_shift_right)
     cp("v", A("xpb", 1, 33), A("xbo"))
+    shift("xpb", "ps1", "b")
     runs("xpb", "ps1", "b", "offb", "exb", "cb2")
     mm(A("ps2"), A("mbb"), A("exb"), True, True, "g_mb")
     cp("s", A("mb"), A("ps2"))
     ts(A("xao"), A("pint"), 2047, OPS.bitwise_and)
-    slots(A("xao"), 32, ("u1", "u2", "u3", "u4", "u5"), A("xaou"))
+    slots(A("xao"), 32, ("u1", "u2", "u3", "u4", "u5", "u6"), A("xaou"))
 
     arrival("land5", 32, "arr5")
     dma("y", ext(T["ya"][:, :], "ya"), A("yat", 0, 2048, 0, 16), "d_ya",
         [X(None, "land5", 32 * q, 32 * q + 32) for q in near])
-    where5 = [(4, 0), (4, 1), (5, 0), (5, 1), (6, 0), (6, 1), (7, 0), (3, 0)]
-    for w in waves:
-        for h in range(8):
-            for q in w:
-                k, c = where5[h][0], 256 * where5[h][1] + 32 * q
-                mm(A("ps%d" % k, c, c + 64), A("repf", 128 * h, 128 * h + 128), A("land5", 32 * q, 32 * q + 64),
-                   True, True, "g_u%d" % k)
-    for q, k, h, n in (("v", 4, 0, 512), ("s", 5, 2, 512), ("v", 6, 4, 512), ("s", 7, 6, 256), ("v", 3, 7, 256)):
-        cp(q, A("ta", 256 * h, 256 * h + n), A("ps%d" % k, 0, n))
+    for q, k, h0, h1, e in ((p_own, 4, 0, 8, "s"), (p_far[0], 5, 0, 8, "v"), (p_far[1], 6, 0, 8, "s"),
+                            (p_near, 7, 0, 4, "v"), (p_near, 3, 4, 8, "s")):
+        for h in range(h0, h1):
+            mm(A("ps%d" % k, 64 * (h - h0), 64 * (h - h0) + 64), A("repf", 128 * h, 128 * h + 128),
+               A("land5", 32 * q, 32 * q + 64), True, True, "g_u%d" % k)
+        cp(e, A("ta", 256 * q + 64 * h0, 256 * q + 64 * h1), A("ps%d" % k, 0, 64 * (h1 - h0)))
     tt(A("wb"), ind(A("ta"), A("xaou")), A("vcp"), OPS.mult)
     scan(A("rb"), A("mb"), A("wb"))
     cp("v", ind(A("w3"), A("offb")), A("rb"))

@@ -4,38 +4,37 @@ from concourse.mybir import AluOpType, ActivationFunctionType
 
 OPS = AluOpType
 COPY = ActivationFunctionType.Copy
-F, BFT, I32, U16 = "float32", "bfloat16", "int32", "uint16"
+F, BFT, I32, U16, F16 = "float32", "bfloat16", "int32", "uint16", "float16"
 
 NDUMP = 640
 SCRATCH = {}
 for _n, _c, _t in [
         ("i1", 128, I32), ("i1b", 128, I32), ("i2", 8, I32), ("i2b", 8, I32), ("i4", 128, I32),
         ("i4b", 128, I32), ("i5", 128, I32), ("ki", 32, I32), ("kk", 32, U16), ("dj", 32, F),
-        ("mk", 8, F), ("i16", 512, F), ("z", 144, F), ("ident", 128, F), ("mbf", 128, F), ("mbb", 128, BFT),
-        ("e8", 128, F), ("n1", 128, F), ("n2", 128, F), ("p1", 128, F), ("p2", 128, F),
-        ("repb", 1024, BFT), ("repf", 1024, F), ("cb", 256, BFT),
-        ("tf", 4096, BFT), ("far", 2048, BFT), ("v8", 512, F), ("v16", 512, F), ("xi", 128, I32), ("ln", 32, I32),
-        ("lau", 16, U16), ("lbu", 16, U16), ("lu", 32, U16), ("lta", 16, U16), ("t1", 64, I32), ("t2", 64, I32),
-        ("t3", 64, I32), ("t4", 64, I32), ("t5", 64, I32), ("t6", 64, I32), ("xu", 64, U16),
-        ("obu", 32, U16), ("xpa", 34, F), ("xpb", 34, F),
+        ("mk", 8, F), ("i16", 512, F), ("z", 144, F), ("z16", 144, F16), ("ident", 128, F), ("mbf", 128, F),
+        ("mbb", 128, BFT), ("e8", 128, F), ("n1", 128, F), ("n2", 128, F), ("p1", 128, F), ("p2", 128, F),
+        ("repb", 1024, BFT), ("repf", 1024, F),
+        ("tf", 2048, BFT), ("far", 2048, BFT), ("v8", 512, F), ("v16", 512, F), ("xi", 128, I32), ("ln", 32, I32),
+        ("lra", 16, U16), ("lau", 16, U16), ("lbu", 16, U16), ("lu", 32, U16), ("lf", 128, U16),
+        ("xu", 64, U16), ("obu", 32, U16), ("xpa", 34, F), ("xpb", 34, F),
+        ("r1", 32, I32), ("r2", 32, I32), ("r3", 32, I32), ("r4", 32, I32), ("r5", 32, I32), ("r6", 32, I32),
+        ("pl", 32, F),
         ("ea", 32, F), ("ca", 32, F), ("da", 32, F), ("fma", 32, F), ("ga", 32, F), ("offa", 32, U16),
         ("eb", 32, F), ("cb2", 32, F), ("db", 32, F), ("fmb", 32, F), ("gb", 32, F), ("offb", 32, U16),
-        ("exa", 512, BFT), ("exb", 512, BFT), ("ma", 512, F), ("mb", 512, F),
-        ("pk0", 32, F), ("pk", 32, F), ("exp", 512, F), ("fp", 512, F), ("pm", 512, F), ("pint", 32, I32),
+        ("exa", 512, BFT), ("exb", 512, BFT),
+        ("pk0", 32, F), ("pk", 32, F), ("exp", 512, F), ("fp", 512, F), ("pm", 512, F), ("pm2", 256, F),
+        ("pm4", 128, F), ("pm8", 64, F), ("pint", 32, I32),
         ("xao", 32, I32), ("xbo", 32, I32), ("u1", 32, I32), ("u2", 32, I32), ("u3", 32, I32), ("u4", 32, I32),
         ("u5", 32, I32), ("u6", 32, I32), ("xaou", 32, U16),
-        ("s1", 512, BFT), ("tb", 2048, BFT), ("tc", 2048, BFT), ("vc", 512, F), ("vcp", 512, F), ("wa", 512, F),
-        ("ra", 512, F), ("w1", 2048 + NDUMP, F), ("s3", 256, F), ("q3", 256, F), ("w2", 2048, F), ("yat", 2048, F),
-        ("s5", 256, F), ("land3", 256, F), ("land5", 256, F), ("land6", 256, F), ("ta", 2048, F), ("wb", 512, F),
-        ("rb", 512, F), ("w3", 2048 + NDUMP, F), ("s6", 256, F), ("q6", 256, F), ("w4", 2048, F), ("y1", 256, F),
-        ("y2", 256, F)]:
+        ("s1", 512, BFT), ("land1", 512, BFT), ("tb", 2048, BFT), ("tc", 2048, BFT), ("vc", 512, F), ("vcp", 512, F),
+        ("wa", 512, F), ("ra", 512, F), ("w1", 2048 + NDUMP, F), ("s3", 224, F), ("q3", 256, F), ("fan", 256, F),
+        ("w2", 2048, F), ("gt", 2048, F), ("ya2", 256, F),
+        ("s5", 224, F), ("land3", 256, F), ("land5", 256, F), ("land6", 256, F), ("ta", 2048, F), ("wb", 512, F),
+        ("rb", 512, F), ("w3", 2048 + NDUMP, F), ("s6", 224, F), ("q6", 256, F), ("w4", 2048, F), ("yb2", 256, F)]:
     SCRATCH[_n] = ("sbuf", [128, _c], _t)
-SCRATCH["ll"] = ("sbuf", [128, 3, 8, 2], I32)
-SCRATCH["llf"] = ("sbuf", [128, 8, 4], F)
-SCRATCH["laf"] = ("sbuf", [128, 8, 2], F)
-SCRATCH["rr"] = ("sbuf", [128, 8, 8, 4], F)
-SCRATCH["rra"] = ("sbuf", [128, 8, 8, 2], F)
-SCRATCH["land1"] = ("sbuf", [128, 16, 32], BFT)
+SCRATCH["ll"] = ("sbuf", [128, 8, 4], I32)
+SCRATCH["rr"] = ("sbuf", [128, 8, 8, 4], F16)
+SCRATCH["rra"] = ("sbuf", [128, 128], F)
 for _k in range(8):
     SCRATCH["ps%d" % _k] = ("psum", [128, 512], F)
 NSEM = 130
@@ -115,6 +114,9 @@ def rank_program(g, core, T, topo):
     def fill(out, c, grp=None):
         record("v", lambda: g.vector.memset(out[0], c), [out], [], grp)
 
+    def turn(out, in_):
+        record("v", lambda: g.vector.transpose(out[0], in_[0]), [out], [in_])
+
     def mm(out, l, r, start, stop, grp):
         record("t", lambda: g.tensor.matmul(out[0], l[0], r[0], start, stop), [out], [l, r], grp)
 
@@ -163,15 +165,15 @@ def rank_program(g, core, T, topo):
             return share(q, far, off_chip)
         if q in near:
             return share(q, near, off_chip)
-        return on_chip[:len(on_chip) // 2]
+        return on_chip[:len(on_chip) // 4]
 
     sent = [0]
 
     def kind(q):
         return "f" if q in far else "n" if q in near else "s"
 
-    def send(src, width, dst, arr, early):
-        for dests in (far + sib, near) if early else (far, near + sib):
+    def send(src, width, dst, arr):
+        for dests in (far, near + sib):
             tr, rd = [], []
             for q in dests:
                 d = order.index(q)
@@ -181,7 +183,8 @@ def rank_program(g, core, T, topo):
                 es = engines_for(q)
                 sent[0] += len(es)
                 tr.append(RemoteDMATransfer(dst_ids=[DstId(rid=rid, pnc=pid)], dma_engine_mask=sum(1 << e for e in es),
-                                            remote_sem=T.sem[arr + kind(q)], srcs=[s[0]], dsts=[dst(me)]))
+                                            remote_sem=T.sem[arr + kind(q)], srcs=[s[0]],
+                                            dsts=[T[dst][:, width * me:width * me + width]]))
             record("g", lambda tr=tr: g.remote_dma_fused(tr, local_sem=T.sem["sent"]), [], rd)
 
     def arrival(n, width, arr):
@@ -189,23 +192,20 @@ def rank_program(g, core, T, topo):
             regs = [(n, 0, 128, q * width, (q + 1) * width) for q in srcs]
             record("in_" + arr + w, None, [(None, regs)], [], fixed=(arr + w, sum(len(engines_for(q)) for q in srcs)))
 
-    dma("y", X(T["ll"][:, 0, :, :], "ll", 0, 16), ext(T["lb"][:, :], "lb"), "d_l")
-    dma("y", X(T["ll"][:, 1, :, :], "ll", 16, 32), ext(T["lc"][:, :], "lc"), "d_l")
-    for h in range(8):
-        dma("s", A("cb", 0, 256, 16 * h, 16 * h + 16), ext(T["fc"][:, 256 * h:256 * h + 256], "fc"), "d_cb")
+    dma("y", X(T["ll"][:, 0:4, :], "ll", 0, 16), ext(T["lb"][:, :], "lb"), "d_l")
+    dma("s", X(T["ll"][:, 4:8, :], "ll", 16, 32), ext(T["lc"][:, :], "lc"), "d_l")
     for k in range(8):
-        dma("s" if k > 5 else "y", A("tf", 0, 2048, 16 * k, 16 * k + 16), ext(T["fb"][:, :], "fb"), "d_tf")
+        n = "fb" if k < 4 else "fc"
+        dma("ys"[k % 2], A("tf", 0, 2048, 16 * k, 16 * k + 16), ext(T[n][:, :], n), "d_tf")
     for k, n in enumerate(("xa", "xb", "xc", "ob")):
         dma("y", A("xi", 32 * k, 32 * k + 32), ext(T[n][:, :], n), "d_x")
     dma("y", A("v8", 0, 512, 0, 8), ext(T["v"][:, :], "v"), "d_x")
-    dma("y", X(T["ll"][:, 2, :, :], "ll", 32, 48), ext(T["la"][:, :], "la"), "d_x")
     dma("y", A("ln", 0, 16), ext(T["la"][:, :], "la"), "d_x")
     dma("y", A("ln", 16, 32), ext(T["lb"][:, :], "lb"), "d_x")
 
     iota("i2", 8, [[-16, 8]], 0, 1)
     iota("i1", 128, [[0, 8], [-1, 16]], 16, 1)
     iota("i4", 128, [[-16, 8], [0, 16]], 0, 1)
-    iota("ki", 32, [[1, 32]], 0, 0)
     iota("i5", 128, [[1, 8], [0, 16]], 0, -1)
     iota("dj", 32, [[16, 32]], 2048, 1, True)
     fill(A("z"), 0.0)
@@ -214,57 +214,41 @@ def rank_program(g, core, T, topo):
     ts(A("i1b"), A("i1"), 15, OPS.bitwise_and)
     ts(A("i16", 0, 128), A("i1b"), 0, OPS.is_equal)
     cp("v", A("z", 112, 128), A("i16", 0, 16))
-    fill(A("xpa"), -1.0)
-    fill(A("xpb"), -1.0)
-    cp("v", A("kk"), A("ki"))
+    cp("v", A("z16"), A("z"))
     ts(A("i4b"), A("i4"), 4, OPS.arith_shift_right)
     ts(A("mbf"), A("i4b"), 0, OPS.is_equal)
+    cp("v", A("mbb"), A("mbf"))
+    fill(A("xpa"), -1.0)
+    fill(A("xpb"), -1.0)
+    ts(A("e8"), A("i5"), 0, OPS.is_equal)
     for n, k in (("n1", -1), ("n2", 15), ("p1", 1), ("p2", -15)):
         pick(n, k)
     for h in range(8):
         scaled(A("repb", 128 * h, 128 * h + 128), A("i16", 0, 128), A("mk", h, h + 1), "g_repb")
 
-    for h in range(8):
-        mm(A("ps%d" % (h // 2), 256 * (h % 2), 256 * (h % 2) + 256), A("repb", 128 * h, 128 * h + 128), A("cb"),
-           True, True, "g_c%d" % (h // 2))
-    ll, llf, rr = T["ll"], T["llf"], T["rr"]
-    cp("v", X(llf[:, :, 0:2], "llf", 0, 1), X(ll[:, 0, :, :], "ll", 0, 16))
-    ts(X(llf[:, :, 2:4], "llf", 1, 2), X(ll[:, 1, :, :], "ll", 16, 32), 2048, OPS.add)
     for d in range(8):
         r = order[d]
-        ts(X(rr[:, :, d, :], "rr", d, d + 1), X(llf[:, :, :], "llf", 0, 2), A("mk", r, r + 1), OPS.mult, grp="g_rr")
-
-    def to_blocked(ps, n, src, grp):
-        for h in range(8):
-            b = 32 * (h // 2)
-            mm((T[ps][b:b + 32, 0:n], [(ps, b, b + 32, 0, n)]), A("z", 112 - 16 * (h % 2), 144 - 16 * (h % 2)),
-               X(T[src][:, h, :, :], src, 0, 8), h % 2 == 0, h % 2 == 1, grp)
-
-    to_blocked("ps4", 32, "rr", "g_lt")
-    for k in range(4):
-        cp("sssv"[k], A("tf", 2048 + 512 * k, 2560 + 512 * k), A("ps%d" % k))
+        ts(X(T["rr"][:, :, d, :], "rr", d, d + 1), X(T["ll"][:, :, :], "ll", 0, 32), A("mk", r, r + 1), OPS.mult,
+           grp="g_rr")
+    for h in range(8):
+        b = 32 * (h // 2)
+        mm((T["ps4"][b:b + 32, 0:32], [("ps4", b, b + 32, 0, 32)]), A("z16", 112 - 16 * (h % 2), 144 - 16 * (h % 2)),
+           X(T["rr"][:, h, :, :], "rr", 0, 8), h % 2 == 0, h % 2 == 1, "g_lt")
     cp("v", A("lu"), A("ps4", 0, 32))
     cp("v", A("s1", 0, 256), ind(A("tf"), A("lu", 0, 16)))
     cp("s", A("s1", 256, 512), ind(A("tf"), A("lu", 16, 32)))
-
-    land1 = T["land1"]
-
-    def at1(q):
-        return land1[:, 2 * q:2 * q + 2, :]
-
-    send("s1", 64, at1, "arr1", True)
+    send("s1", 64, "land1", "arr1")
     pick("ident", 0)
     iota("w1", 2048, [[0, 2048]], 0, 0, True)
+    rep, zero = A("repf"), A("w1", 0, 1024)
+    record("g", lambda: g.affine_select(rep[0], zero[0], [[-16, 8], [0, 8], [-1, 16]], OPS.not_equal, 1.0, 0, 1),
+           [rep], [zero])
     iota("w2", 2048, [[0, 2048]], 0, 0, True)
-    for f in range(2):
-        cp("s", X(land1[:, 2 * me + f, :], "land1", 2 * me + f, 2 * me + f + 1),
-           A("s1", 448 + 32 * f, 480 + 32 * f), "g_own1")
+    cp("s", A("land1", 64 * me, 64 * me + 64), A("s1", 448, 512))
 
     for k in range(1, 4):
         cp("s", A("i16", 128 * k, 128 * k + 128), A("i16", 0, 128), "g_i16")
     cp("v", A("xpa", 1, 33), A("xi", 0, 32))
-    ts(A("e8"), A("i5"), 0, OPS.is_equal)
-    ts(A("pk0"), A("xi", 32, 64), 2048, OPS.mult)
 
     def shift(xp, ps, s):
         mm(A(ps, 0, 32), A("n1"), A(xp, 1, 33), True, False, "g_n" + s)
@@ -272,86 +256,88 @@ def rank_program(g, core, T, topo):
         mm(A(ps, 32, 64), A("p1"), A(xp, 1, 33), True, False, "g_n" + s)
         mm(A(ps, 32, 64), A("p2"), A(xp, 0, 32), False, True, "g_n" + s)
 
-    def runs(xp, ps, s, off, ex, c):
-        tt(A("d" + s), A(xp, 1, 33), A("dj"), OPS.subtract)
-        tt(A(c), A(ps, 32, 64), A(xp, 1, 33), OPS.is_equal)
+    def ends(xp, ps, s, off):
         tt(A("e" + s), A(ps, 0, 32), A(xp, 1, 33), OPS.not_equal)
-        tt(A(ex), ind(A(c), A("kk")), A("i16"), OPS.mult)
         tt(A("fm" + s), A("d" + s), A("e" + s), OPS.mult)
         tt(A("g" + s), A("fm" + s), A("dj"), OPS.add)
         cp("v", A(off), A("g" + s))
 
-    def slots(x, n, t, out):
-        ts(A(t[0], 0, n), x, 5, OPS.arith_shift_right, 7, OPS.bitwise_and)
-        ts(A(t[1], 0, n), x, 8, OPS.arith_shift_right, 1, OPS.bitwise_and)
-        ts(A(t[2], 0, n), A(t[0], 0, n), 32, OPS.mult)
-        ts(A(t[3], 0, n), A(t[1], 0, n), -224, OPS.mult)
-        tt(A(t[4], 0, n), A(t[2], 0, n), x, OPS.add)
-        tt(A(t[5], 0, n), A(t[3], 0, n), A(t[4], 0, n), OPS.add)
-        cp("v", out, A(t[5], 0, n))
+    def spread(out, x, grp):
+        for i in range(16):
+            scaled(A(out, i, 512, step=16), A(x), A("i16", i, i + 1), grp)
 
     shift("xpa", "ps7", "a")
     mm(A("ps5"), A("e8", 0, 128, 0, 8), A("v8", 0, 512, 0, 8), True, True, "g_v")
-    tt(A("pk"), A("pk0"), A("xpa", 1, 33), OPS.add)
+    ts(A("pk0"), A("xi", 32, 64), 2048, OPS.mult)
+    tt(A("da"), A("xpa", 1, 33), A("dj"), OPS.subtract)
+    tt(A("ca"), A("ps7", 32, 64), A("xpa", 1, 33), OPS.is_equal)
     cp("s", A("v16"), A("ps5"))
-    cp("v", A("mbb"), A("mbf"))
-    slots(A("xi", 32, 96), 64, ("t1", "t2", "t3", "t4", "t5", "t6"), A("xu"))
+    spread("exa", "ca", "g_exa")
+    ends("xpa", "ps7", "a", "offa")
+    cp("v", A("xu"), A("xi", 32, 96))
+    tt(A("pk"), A("pk0"), A("xpa", 1, 33), OPS.add)
     cp("v", A("obu"), A("xi", 96, 128))
-    laf = T["laf"]
-    cp("v", X(laf[:, :, :], "laf", 0, 1), X(ll[:, 2, :, :], "ll", 32, 48))
-    runs("xpa", "ps7", "a", "offa", "exa", "ca")
+    cp("v", A("lra"), A("ln", 0, 16))
+    ts(A("r1"), A("ln"), 9, OPS.arith_shift_right)
+    ts(A("r2"), A("ln"), 31, OPS.bitwise_and)
+    ts(A("r5"), A("ln"), 4, OPS.mult)
+    ts(A("r3"), A("r1"), -2016, OPS.mult)
+    ts(A("r4"), A("r2"), -3, OPS.mult)
+    tt(A("r6"), A("r5"), A("r3"), OPS.add)
+    tt(A("pl"), A("r6"), A("r4"), OPS.add)
+    cp("v", A("lau"), A("pl", 0, 16))
 
-    arrival("land1", 2, "arr1")
+    arrival("land1", 64, "arr1")
     for k in range(8):
         dma("y", A("far", 0, 2048, 16 * k, 16 * k + 16), ext(T["fa"][:, :], "fa"), "d_fa",
-            [X(None, "land1", 2 * q, 2 * q + 2) for q in near])
-    for f, q, k, h0, h1, e in ((1, p_own, 0, 0, 8, "v"), (0, p_own, 4, 0, 8, "s"), (1, p_far[0], 1, 0, 8, "v"),
-                               (1, p_far[1], 2, 0, 8, "s"), (0, p_far[0], 5, 0, 8, "v"), (0, p_far[1], 6, 0, 8, "s"),
-                               (1, p_near, 3, 0, 4, "v"), (1, p_near, 0, 4, 8, "s"), (0, p_near, 7, 0, 8, "s")):
-        for h in range(h0, h1):
-            mm(A("ps%d" % k, 64 * (h - h0), 64 * (h - h0) + 64), A("repb", 128 * h, 128 * h + 128),
-               X(land1[:, 2 * q + f:2 * q + 4:2, :], "land1", 2 * q, 2 * q + 4), True, True, "g_t%d%d" % (k, h0))
-        cp(e, A("tb" if f == 0 else "tc", 256 * q + 64 * h0, 256 * q + 64 * h1), A("ps%d" % k, 0, 64 * (h1 - h0)))
+            [A("land1", 64 * q, 64 * q + 64) for q in near])
+    for f, q, n, k, e in ((1, p_own, 2, 0, "v"), (0, p_own, 2, 4, "s"), (1, p_far[0], 2, 1, "v"),
+                          (1, p_far[1], 2, 2, "s"), (0, p_far[0], 2, 5, "v"), (0, p_far[1], 2, 6, "s"),
+                          (1, p_near, 1, 3, "v"), (1, p_near + 1, 1, 0, "s"), (0, p_near, 2, 7, "s")):
+        for i in range(4 * n):
+            w = 128 * (4 * f + i % 4)
+            lo = 64 * (q + i // 4)
+            mm(A("ps%d" % k, 64 * i, 64 * i + 64), A("repb", w, w + 128), A("land1", lo, lo + 64), True, True,
+               "g_t%d%d" % (k, q))
+        cp(e, A("tb" if f == 0 else "tc", 256 * q, 256 * (q + n)), A("ps%d" % k, 0, 256 * n))
     mm(A("ps1"), A("mbb"), A("exa"), True, True, "g_ma")
-    cp("s", A("ma"), A("ps1"))
     tt(A("vc"), ind(A("tc"), A("xu", 32, 64)), A("v16"), OPS.mult)
     tt(A("wa"), ind(A("tb"), A("xu", 0, 32)), A("vc"), OPS.mult)
-    scan(A("ra"), A("ma"), A("wa"))
+    scan(A("ra"), A("ps1"), A("wa"))
     cp("v", ind(A("w1"), A("offa")), A("ra"))
-    for i in range(16):
-        scaled(A("exp", i, 512, step=16), A("pk"), A("i16", i, i + 1), "g_exp")
+    spread("exp", "pk", "g_exp")
     mm(A("ps2"), A("mbf"), A("exp"), True, True, "g_fp")
     cp("s", A("fp"), A("ps2"))
     cp("s", A("vcp"), ind(A("vc"), A("obu")))
+
+    bank = (0, 0, 0, 0, 1, 1, 1, 2)
 
     def add_slabs(w, s, land, arr):
         for d in range(8):
             for b in range(2):
                 c = 32 * (d % 4)
                 k = 2 * order[d] + b
-                mm(A("ps0" if d < 4 else "ps1", c + b, c + 32, step=2), A(w, 128 * k, 128 * k + 128), A("i16", 0, 16),
-                   True, True, "g_%s%d" % (w, d // 4))
+                mm(A("ps%d" % bank[d], c + b, c + 32, step=2), A(w, 128 * k, 128 * k + 128), A("i16", 0, 16),
+                   True, True, "g_%s%d" % (w, bank[d]))
         cp("v", A(s, 0, 128), A("ps0", 0, 128))
-        cp("s", A(s, 128, 256), A("ps1", 0, 128))
-        send(s, 32, lambda q: T[land][:, 32 * q:32 * q + 32], arr, False)
-        cp("s", A(land, 32 * me, 32 * me + 32), A(s, 224, 256))
+        cp("s", A(s, 128, 224), A("ps1", 0, 96))
+        send(s, 32, land, arr)
+        cp("s", A(land, 32 * me, 32 * me + 32), A("ps2", 96, 128))
 
     add_slabs("w1", "s3", "land3", "arr3")
     iota("w3", 2048, [[0, 2048]], 0, 0, True)
-    iota("w4", 2048, [[0, 2048]], 0, 0, True)
 
-    tt(A("pm"), ind(A("fp"), A("obu")), A("i16"), OPS.mult)
-    cp("v", A("lau"), A("ln", 0, 16))
-    cp("v", A("lbu"), A("ln", 16, 32))
+    cp("s", A("fan"), ind(A("far"), A("lra")))
     for d in range(8):
         r = order[d]
-        scaled(X(T["rra"][:, :, d, :], "rra", d, d + 1), X(laf[:, :, :], "laf", 0, 1), A("mk", r, r + 1), grp="g_rra")
-    to_blocked("ps4", 16, "rra", "g_lta")
-    cp("v", A("lta"), A("ps4", 0, 16))
-    for i in range(16):
-        mm(A("ps3", 0, 32), A("ident"), A("pm", i, 512, step=16), i == 0, i == 15, "g_pm")
-    for h in range(8):
-        scaled(A("repf", 128 * h, 128 * h + 128), A("i16", 0, 128), A("mk", h, h + 1), "g_repf")
+        scaled(A("rra", 16 * d, 16 * d + 16), A("pl", 0, 16), A("mk", r, r + 1), "g_rra")
+    mm(A("ps4", 0, 128), A("i16", 0, 128), A("rra"), True, True, "g_lf")
+    tt(A("pm"), ind(A("fp"), A("obu")), A("i16"), OPS.mult)
+    tt(A("pm2"), A("pm", 0, 512, step=2), A("pm", 1, 512, step=2), OPS.add)
+    cp("v", A("lf"), A("ps4", 0, 128))
+    tt(A("pm4"), A("pm2", 0, 256, step=2), A("pm2", 1, 256, step=2), OPS.add)
+    tt(A("pm8"), A("pm4", 0, 128, step=2), A("pm4", 1, 128, step=2), OPS.add)
+    tt(A("pint"), A("pm8", 0, 64, step=2), A("pm8", 1, 64, step=2), OPS.add)
 
     def to_natural(land, q, pa, pb):
         mm(A(pa, 0, 128), A(land, 0, 256, step=2), A("ident"), True, True, "g_n0" + land)
@@ -361,51 +347,77 @@ def rank_program(g, core, T, topo):
 
     arrival("land3", 32, "arr3")
     to_natural("land3", "q3", "ps6", "ps7")
-    cp("v", ind(A("w2"), A("lau")), A("q3"))
-    for k, lo, n in ((0, 0, 512), (1, 512, 512), (2, 1024, 512), (5, 1536, 256), (4, 1792, 256)):
-        mm(A("ps%d" % k, 0, n), A("i16", 0, 128), A("w2", lo, lo + n), True, True, "g_y%d" % k)
-        tt(A("yat", lo, lo + n), A("ps%d" % k, 0, n), A("far", lo, lo + n), OPS.mult)
-    cp("v", A("s5", 0, 128), ind(A("yat"), A("lta", 0, 8)))
-    cp("s", A("s5", 128, 256), ind(A("yat"), A("lta", 8, 16)))
-    send("s5", 32, lambda q: T["land5"][:, 32 * q:32 * q + 32], "arr5", True)
-    cp("s", A("land5", 32 * me, 32 * me + 32), A("s5", 224, 256))
+    tt(ind(A("w2"), A("lau")), A("q3"), A("fan"), OPS.mult)
+    for d in range(8):
+        cp("vsvsvssv"[d], A("gt", 256 * d, 256 * d + 256), ind(A("w2"), A("lf", 16 * d, 16 * d + 16)))
+        for b in range(2):
+            c = 32 * (d % 4) + 16 * b
+            mm(A("ps%d" % bank[d], c, c + 16), A("gt", 256 * d + 128 * b, 256 * d + 128 * b + 128), A("i16", 0, 16),
+               True, True, "g_m%d" % bank[d])
+        if d == 3:
+            turn(A("s5", 0, 128), A("ps0", 0, 128))
+    turn(A("s5", 128, 224), A("ps1", 0, 96))
+    turn(A("land5", 32 * me, 32 * me + 32), A("ps2", 96, 128))
+    send("s5", 32, "land5", "arr5")
+    iota("w4", 2048, [[0, 2048]], 0, 0, True)
 
-    cp("v", A("pint"), A("ps3", 0, 32))
     ts(A("xbo"), A("pint"), 11, OPS.arith_shift_right)
     cp("v", A("xpb", 1, 33), A("xbo"))
     shift("xpb", "ps1", "b")
-    runs("xpb", "ps1", "b", "offb", "exb", "cb2")
-    mm(A("ps2"), A("mbb"), A("exb"), True, True, "g_mb")
-    cp("s", A("mb"), A("ps2"))
     ts(A("xao"), A("pint"), 2047, OPS.bitwise_and)
-    slots(A("xao"), 32, ("u1", "u2", "u3", "u4", "u5", "u6"), A("xaou"))
+    tt(A("db"), A("xpb", 1, 33), A("dj"), OPS.subtract)
+    tt(A("cb2"), A("ps1", 32, 64), A("xpb", 1, 33), OPS.is_equal)
+    spread("exb", "cb2", "g_exb")
+    ends("xpb", "ps1", "b", "offb")
+    ts(A("u1"), A("xao"), 5, OPS.arith_shift_right, 7, OPS.bitwise_and)
+    ts(A("u2"), A("xao"), 8, OPS.arith_shift_right, 1, OPS.bitwise_and)
+    ts(A("u3"), A("u1"), 32, OPS.mult)
+    ts(A("u4"), A("u2"), -224, OPS.mult)
+    tt(A("u5"), A("u3"), A("xao"), OPS.add)
+    tt(A("u6"), A("u4"), A("u5"), OPS.add)
+    cp("v", A("xaou"), A("u6"))
 
     arrival("land5", 32, "arr5")
-    dma("y", ext(T["ya"][:, :], "ya"), A("yat", 0, 2048, 0, 16), "d_ya",
-        [X(None, "land5", 32 * q, 32 * q + 32) for q in near])
-    for q, k, h0, h1, e in ((p_own, 4, 0, 8, "s"), (p_far[0], 5, 0, 8, "v"), (p_far[1], 6, 0, 8, "s"),
-                            (p_near, 7, 0, 4, "v"), (p_near, 3, 4, 8, "s")):
-        for h in range(h0, h1):
-            mm(A("ps%d" % k, 64 * (h - h0), 64 * (h - h0) + 64), A("repf", 128 * h, 128 * h + 128),
+    for q, k, u0, u1, e in ((p_far[0], 5, 0, 8, "v"), (p_far[1], 6, 0, 8, "s"), (p_own, 4, 0, 8, "v"),
+                            (p_near, 7, 0, 4, "s"), (p_near, 3, 4, 6, "v"), (p_near, 0, 6, 8, "s")):
+        for u in range(u0, u1):
+            h = 2 * (u % 4) + u // 4
+            mm(A("ps%d" % k, 64 * (u - u0), 64 * (u - u0) + 64), A("repf", 128 * h, 128 * h + 128),
                A("land5", 32 * q, 32 * q + 64), True, True, "g_u%d" % k)
-        cp(e, A("ta", 256 * q + 64 * h0, 256 * q + 64 * h1), A("ps%d" % k, 0, 64 * (h1 - h0)))
+        cp(e, A("ta", 256 * q + 64 * u0, 256 * q + 64 * u1), A("ps%d" % k, 0, 64 * (u1 - u0)))
+    mm(A("ps2"), A("mbb"), A("exb"), True, True, "g_mb")
+
+    def sum_own(w, half, ps, grp):
+        for i in range(4):
+            for k in range(2):
+                lo = 1024 * k + 128 * (4 * half + i)
+                mm(A(ps, 32 * i + 16 * k, 32 * i + 16 * k + 16), A(w, lo, lo + 128), A("i16", 0, 16), True, True,
+                   "g_%s%d" % (grp, half))
+
+    def store(y, out, qs):
+        for h in range(8):
+            dma(qs[h % len(qs)], ext(T[out][:, 256 * h:256 * h + 256], "%s%d" % (out, h)),
+                A(y, 0, 256, 16 * h, 16 * h + 16), "d_" + out)
+
+    sum_own("w2", 0, "ps4", "ya")
     tt(A("wb"), ind(A("ta"), A("xaou")), A("vcp"), OPS.mult)
-    scan(A("rb"), A("mb"), A("wb"))
+    scan(A("rb"), A("ps2"), A("wb"))
     cp("v", ind(A("w3"), A("offb")), A("rb"))
+    turn(A("ya2", 0, 128), A("ps4", 0, 128))
 
     add_slabs("w3", "s6", "land6", "arr6")
+    sum_own("w2", 1, "ps5", "ya")
+    turn(A("ya2", 128, 256), A("ps5", 0, 128))
+    store("ya2", "ya", "y")
+    cp("v", A("lbu"), A("pl", 16, 32))
     arrival("land6", 32, "arr6")
     to_natural("land6", "q6", "ps2", "ps3")
     cp("v", ind(A("w4"), A("lbu")), A("q6"))
-    for k in range(16):
-        mm(A("ps%d" % (4 + k // 8), k % 8, 128, step=8), A("w4", 128 * k, 128 * k + 128), A("i16", 0, 16), True, True,
-           "g_z%d" % (k // 8))
-    for k in range(2):
-        cp("vs"[k], A("y1", 128 * k, 128 * k + 128), A("ps%d" % (4 + k), 0, 128))
-        mm(A("ps%d" % (6 + k), 0, 128), A("y1", 128 * k, 128 * k + 128), A("ident"), True, True, "g_b%d" % k)
-        cp("vs"[k], A("y2", 128 * k, 128 * k + 128), A("ps%d" % (6 + k), 0, 128))
-        dma("ys"[k], ext(T["yb"][:, 1024 * k:1024 * k + 1024], "yb%d" % k), A("y2", 128 * k, 128 * k + 128), "d_yb%d" % k)
-    record("y", None, [], [(None, [("ext_" + n, 0, 128, 0, 1) for n in ("ya", "yb0", "yb1")])])
+    for half in range(2):
+        sum_own("w4", half, "ps%d" % (6 + half), "yb")
+        turn(A("yb2", 128 * half, 128 * half + 128), A("ps%d" % (6 + half), 0, 128))
+    store("yb2", "yb", "ys")
+    record("y", None, [], [(None, [("ext_%s%d" % (n, h), 0, 128, 0, 1) for n in ("ya", "yb") for h in range(8)])])
 
     bits = [0] * len(ops)
     known = {}

@@ -15,10 +15,9 @@ for _n, _c, _t in [
         ("mbb", 128, BFT), ("e8", 128, F), ("n1", 128, F), ("n2", 128, F), ("p1", 128, F), ("p2", 128, F),
         ("repb", 1024, BFT), ("repf", 1024, F),
         ("tf", 2048, BFT), ("far", 2048, BFT), ("v8", 512, F), ("v16", 512, F), ("xi", 128, I32), ("ln", 32, I32),
-        ("lra", 16, U16), ("lau", 16, U16), ("lbu", 16, U16), ("lu", 32, U16), ("lf", 128, U16),
+        ("laf", 16, F), ("lau", 16, U16), ("lbu", 16, U16), ("lu", 32, U16), ("lf", 128, U16),
         ("xu", 64, U16), ("obu", 32, U16), ("xpa", 34, F), ("xpb", 34, F),
-        ("r1", 32, I32), ("r2", 32, I32), ("r3", 32, I32), ("r4", 32, I32), ("r5", 32, I32), ("r6", 32, I32),
-        ("pl", 32, F),
+        ("r1", 16, I32), ("r2", 16, I32), ("r3", 16, I32), ("r4", 16, I32), ("r5", 16, I32), ("r6", 16, I32),
         ("ea", 32, F), ("ca", 32, F), ("da", 32, F), ("fma", 32, F), ("ga", 32, F), ("offa", 32, U16),
         ("eb", 32, F), ("cb2", 32, F), ("db", 32, F), ("fmb", 32, F), ("gb", 32, F), ("offb", 32, U16),
         ("exa", 512, BFT), ("exb", 512, BFT),
@@ -28,7 +27,7 @@ for _n, _c, _t in [
         ("u5", 32, I32), ("u6", 32, I32), ("xaou", 32, U16),
         ("s1", 512, BFT), ("land1", 512, BFT), ("tb", 2048, BFT), ("tc", 2048, BFT), ("vc", 512, F), ("vcp", 512, F),
         ("wa", 512, F), ("ra", 512, F), ("w1", 2048 + NDUMP, F), ("s3", 224, F), ("q3", 256, F), ("fan", 256, F),
-        ("w2", 2048, F), ("gt", 2048, F), ("ya2", 256, F),
+        ("w2", 2048, F), ("gt", 2048, F), ("ya1", 256, F), ("ya2", 256, F),
         ("s5", 224, F), ("land3", 256, F), ("land5", 256, F), ("land6", 256, F), ("ta", 2048, F), ("wb", 512, F),
         ("rb", 512, F), ("w3", 2048 + NDUMP, F), ("s6", 224, F), ("q6", 256, F), ("w4", 2048, F), ("yb2", 256, F)]:
     SCRATCH[_n] = ("sbuf", [128, _c], _t)
@@ -38,7 +37,7 @@ SCRATCH["rra"] = ("sbuf", [128, 128], F)
 for _k in range(8):
     SCRATCH["ps%d" % _k] = ("psum", [128, 512], F)
 NSEM = 130
-SEMAPHORES = ["e%d" % k for k in range(NSEM)] + ["arr%d%s" % (k, s) for k in (1, 3, 5, 6) for s in "fsn"] + ["sent"]
+SEMAPHORES = ["e%d" % k for k in range(NSEM)] + ["arr%d%s" % (k, s) for k in (1, 3, 5, 6) for s in "fhsn"] + ["sent"]
 
 
 def rank_program(g, core, T, topo):
@@ -142,55 +141,60 @@ def rank_program(g, core, T, topo):
         return (ap, [("ext_" + n, 0, 128, 0, 1)])
 
     ranks = range(len(cores))
-    sib = [q for q in ranks if q != me and topo.chip(cores[q]) == here]
-    near = [q for q in ranks if topo.same_plane(topo.chip(cores[q]), here)]
-    far = [q for q in ranks if q != me and q not in sib and q not in near]
-    order = far + near + sib + [me]
 
-    def pairs(qs):
-        return sorted(q for q in qs if q + 1 in qs and topo.chip(cores[q]) == topo.chip(cores[q + 1]))
+    def chip(q):
+        return topo.chip(cores[q])
 
-    p_own, p_far, p_near = pairs(sib + [me])[0], pairs(far), pairs(near)[0]
+    def row(q):
+        return len([p for p in ranks if p < q and topo.same_plane(chip(p), chip(q))])
 
-    def share(q, dests, engines):
-        n = len(engines) // len(dests)
-        i = dests.index(q)
-        return engines[i * n:(i + 1) * n]
+    sib = [q for q in ranks if q != me and chip(q) == here]
+    near = [q for q in ranks if topo.same_plane(chip(q), here)]
+    others = [q for q in ranks if q != me and q not in sib and q not in near]
+    far0 = [q for q in others if row(q) == row(me)]
+    far1 = [q for q in others if q not in far0]
+    order = far0 + far1 + sib + near + [me]
+    p_own, p_far0, p_far1, p_near = min(sib + [me]), min(far0), min(far1), min(near)
+    kinds = (("s", sib), ("f", far0), ("h", far1), ("n", near))
 
-    off_chip = topo.engines(core, cores[far[0]])
+    off_chip = topo.engines(core, cores[others[0]])
     on_chip = [e for e in topo.engines(core, cores[sib[0]]) if e not in off_chip]
 
-    def engines_for(q):
-        if q in far:
-            return share(q, far, off_chip)
-        if q in near:
-            return share(q, near, off_chip)
-        return on_chip[:len(on_chip) // 4]
+    def engines_for(q, dests):
+        if q in sib:
+            return on_chip[:len(on_chip) // 2]
+        dests = [d for d in dests if d not in sib]
+        n = len(off_chip) // len(dests)
+        i = dests.index(q)
+        return off_chip[i * n:(i + 1) * n]
 
     sent = [0]
 
-    def kind(q):
-        return "f" if q in far else "n" if q in near else "s"
-
-    def send(src, width, dst, arr):
-        for dests in (far, near + sib):
+    def send(src, width, dst, arr, calls):
+        for dests in calls:
             tr, rd = [], []
             for q in dests:
                 d = order.index(q)
                 s = A(src, d * width, (d + 1) * width)
                 rd.append(s)
                 rid, pid = topo.addr(cores[q])[:2]
-                es = engines_for(q)
+                es = engines_for(q, dests)
                 sent[0] += len(es)
+                w = [k for k, qs in kinds if q in qs][0]
                 tr.append(RemoteDMATransfer(dst_ids=[DstId(rid=rid, pnc=pid)], dma_engine_mask=sum(1 << e for e in es),
-                                            remote_sem=T.sem[arr + kind(q)], srcs=[s[0]],
+                                            remote_sem=T.sem[arr + w], srcs=[s[0]],
                                             dsts=[T[dst][:, width * me:width * me + width]]))
             record("g", lambda tr=tr: g.remote_dma_fused(tr, local_sem=T.sem["sent"]), [], rd)
 
-    def arrival(n, width, arr):
-        for srcs, w in ((sib, "s"), (far, "f"), (near, "n")):
+    def arrival(n, width, arr, calls):
+        for w, srcs in kinds:
             regs = [(n, 0, 128, q * width, (q + 1) * width) for q in srcs]
-            record("in_" + arr + w, None, [(None, regs)], [], fixed=(arr + w, sum(len(engines_for(q)) for q in srcs)))
+            num = sum(len(engines_for(q, dests)) for dests in calls for q in dests if q in srcs)
+            record("in_" + arr + w, None, [(None, regs)], [], fixed=(arr + w, num))
+
+    calls1 = (far0 + far1, near + sib)
+    calls3 = (far0, far1, near + sib)
+    calls5 = (far0, far1 + sib, near)
 
     dma("y", X(T["ll"][:, 0:4, :], "ll", 0, 16), ext(T["lb"][:, :], "lb"), "d_l")
     dma("s", X(T["ll"][:, 4:8, :], "ll", 16, 32), ext(T["lc"][:, :], "lc"), "d_l")
@@ -208,19 +212,16 @@ def rank_program(g, core, T, topo):
     iota("i4", 128, [[-16, 8], [0, 16]], 0, 1)
     iota("i5", 128, [[1, 8], [0, 16]], 0, -1)
     iota("dj", 32, [[16, 32]], 2048, 1, True)
+    iota("ki", 32, [[1, 32]], 0, 0)
     fill(A("z"), 0.0)
     ts(A("i2b"), A("i2"), 4, OPS.arith_shift_right)
     ts(A("mk"), A("i2b"), 0, OPS.is_equal)
     ts(A("i1b"), A("i1"), 15, OPS.bitwise_and)
     ts(A("i16", 0, 128), A("i1b"), 0, OPS.is_equal)
     cp("v", A("z", 112, 128), A("i16", 0, 16))
-    cp("v", A("z16"), A("z"))
     ts(A("i4b"), A("i4"), 4, OPS.arith_shift_right)
+    cp("v", A("z16"), A("z"))
     ts(A("mbf"), A("i4b"), 0, OPS.is_equal)
-    cp("v", A("mbb"), A("mbf"))
-    fill(A("xpa"), -1.0)
-    fill(A("xpb"), -1.0)
-    ts(A("e8"), A("i5"), 0, OPS.is_equal)
     for n, k in (("n1", -1), ("n2", 15), ("p1", 1), ("p2", -15)):
         pick(n, k)
     for h in range(8):
@@ -234,10 +235,15 @@ def rank_program(g, core, T, topo):
         b = 32 * (h // 2)
         mm((T["ps4"][b:b + 32, 0:32], [("ps4", b, b + 32, 0, 32)]), A("z16", 112 - 16 * (h % 2), 144 - 16 * (h % 2)),
            X(T["rr"][:, h, :, :], "rr", 0, 8), h % 2 == 0, h % 2 == 1, "g_lt")
+    fill(A("xpa"), -1.0)
+    cp("v", A("mbb"), A("mbf"))
     cp("v", A("lu"), A("ps4", 0, 32))
+    fill(A("xpb"), -1.0)
+    cp("v", A("kk"), A("ki"))
+    ts(A("e8"), A("i5"), 0, OPS.is_equal)
     cp("v", A("s1", 0, 256), ind(A("tf"), A("lu", 0, 16)))
     cp("s", A("s1", 256, 512), ind(A("tf"), A("lu", 16, 32)))
-    send("s1", 64, "land1", "arr1")
+    send("s1", 64, "land1", "arr1", calls1)
     pick("ident", 0)
     iota("w1", 2048, [[0, 2048]], 0, 0, True)
     rep, zero = A("repf"), A("w1", 0, 1024)
@@ -272,28 +278,21 @@ def rank_program(g, core, T, topo):
     tt(A("da"), A("xpa", 1, 33), A("dj"), OPS.subtract)
     tt(A("ca"), A("ps7", 32, 64), A("xpa", 1, 33), OPS.is_equal)
     cp("s", A("v16"), A("ps5"))
-    spread("exa", "ca", "g_exa")
     ends("xpa", "ps7", "a", "offa")
     cp("v", A("xu"), A("xi", 32, 96))
+    tt(A("exa"), ind(A("ca"), A("kk")), A("i16"), OPS.mult)
     tt(A("pk"), A("pk0"), A("xpa", 1, 33), OPS.add)
     cp("v", A("obu"), A("xi", 96, 128))
-    cp("v", A("lra"), A("ln", 0, 16))
-    ts(A("r1"), A("ln"), 9, OPS.arith_shift_right)
-    ts(A("r2"), A("ln"), 31, OPS.bitwise_and)
-    ts(A("r5"), A("ln"), 4, OPS.mult)
-    ts(A("r3"), A("r1"), -2016, OPS.mult)
-    ts(A("r4"), A("r2"), -3, OPS.mult)
-    tt(A("r6"), A("r5"), A("r3"), OPS.add)
-    tt(A("pl"), A("r6"), A("r4"), OPS.add)
-    cp("v", A("lau"), A("pl", 0, 16))
+    cp("v", A("lau"), A("ln", 0, 16))
+    cp("v", A("laf"), A("ln", 0, 16))
 
-    arrival("land1", 64, "arr1")
+    arrival("land1", 64, "arr1", calls1)
     for k in range(8):
         dma("y", A("far", 0, 2048, 16 * k, 16 * k + 16), ext(T["fa"][:, :], "fa"), "d_fa",
             [A("land1", 64 * q, 64 * q + 64) for q in near])
-    for f, q, n, k, e in ((1, p_own, 2, 0, "v"), (0, p_own, 2, 4, "s"), (1, p_far[0], 2, 1, "v"),
-                          (1, p_far[1], 2, 2, "s"), (0, p_far[0], 2, 5, "v"), (0, p_far[1], 2, 6, "s"),
-                          (1, p_near, 1, 3, "v"), (1, p_near + 1, 1, 0, "s"), (0, p_near, 2, 7, "s")):
+    for f, q, n, k, e in ((1, p_own, 2, 0, "s"), (0, p_own, 2, 4, "v"), (1, p_far0, 2, 1, "s"),
+                          (1, p_far1, 2, 2, "v"), (0, p_far0, 2, 5, "s"), (0, p_far1, 2, 6, "v"),
+                          (1, p_near, 1, 3, "s"), (1, p_near + 1, 1, 0, "v"), (0, p_near, 2, 7, "s")):
         for i in range(4 * n):
             w = 128 * (4 * f + i % 4)
             lo = 64 * (q + i // 4)
@@ -310,27 +309,26 @@ def rank_program(g, core, T, topo):
     cp("s", A("fp"), A("ps2"))
     cp("s", A("vcp"), ind(A("vc"), A("obu")))
 
-    bank = (0, 0, 0, 0, 1, 1, 1, 2)
-
     def add_slabs(w, s, land, arr):
-        for d in range(8):
-            for b in range(2):
-                c = 32 * (d % 4)
-                k = 2 * order[d] + b
-                mm(A("ps%d" % bank[d], c + b, c + 32, step=2), A(w, 128 * k, 128 * k + 128), A("i16", 0, 16),
-                   True, True, "g_%s%d" % (w, bank[d]))
-        cp("v", A(s, 0, 128), A("ps0", 0, 128))
-        cp("s", A(s, 128, 224), A("ps1", 0, 96))
-        send(s, 32, land, arr)
-        cp("s", A(land, 32 * me, 32 * me + 32), A("ps2", 96, 128))
+        for qs, k in ((far0, 0), (far1, 1), (near + sib, 2), ([me], 3)):
+            for q in qs:
+                for b in range(2):
+                    c = 32 * (order.index(q) % 4)
+                    mm(A("ps%d" % k, c + b, c + 32, step=2), A(w, 256 * q + 128 * b, 256 * q + 128 * b + 128),
+                       A("i16", 0, 16), True, True, "g_%s%d" % (w, k))
+        cp("v", A(s, 0, 64), A("ps0", 0, 64))
+        cp("v", A(s, 64, 128), A("ps1", 64, 128))
+        cp("s", A(s, 128, 224), A("ps2", 0, 96))
+        send(s, 32, land, arr, calls3)
+        cp("s", A(land, 32 * me, 32 * me + 32), A("ps3", 96, 128))
 
     add_slabs("w1", "s3", "land3", "arr3")
     iota("w3", 2048, [[0, 2048]], 0, 0, True)
 
-    cp("s", A("fan"), ind(A("far"), A("lra")))
+    cp("s", A("fan"), ind(A("far"), A("lau")))
     for d in range(8):
         r = order[d]
-        scaled(A("rra", 16 * d, 16 * d + 16), A("pl", 0, 16), A("mk", r, r + 1), "g_rra")
+        scaled(A("rra", 16 * d, 16 * d + 16), A("laf"), A("mk", r, r + 1), "g_rra")
     mm(A("ps4", 0, 128), A("i16", 0, 128), A("rra"), True, True, "g_lf")
     tt(A("pm"), ind(A("fp"), A("obu")), A("i16"), OPS.mult)
     tt(A("pm2"), A("pm", 0, 512, step=2), A("pm", 1, 512, step=2), OPS.add)
@@ -345,20 +343,25 @@ def rank_program(g, core, T, topo):
         cp("s", A(q, 0, 128), A(pa, 0, 128))
         cp("v", A(q, 128, 256), A(pb, 0, 128))
 
-    arrival("land3", 32, "arr3")
+    arrival("land3", 32, "arr3", calls3)
     to_natural("land3", "q3", "ps6", "ps7")
     tt(ind(A("w2"), A("lau")), A("q3"), A("fan"), OPS.mult)
+    bank = (0, 0, 1, 1, 1, 2, 2, 3)
     for d in range(8):
-        cp("vsvsvssv"[d], A("gt", 256 * d, 256 * d + 256), ind(A("w2"), A("lf", 16 * d, 16 * d + 16)))
+        for lo, hi in ((0, 128), (128, 256)) if d < 2 else ((0, 256),):
+            cp("vsvsvssv"[d], A("gt", 256 * d + lo, 256 * d + hi),
+               ind(A("w2"), A("lf", 16 * d + lo // 16, 16 * d + hi // 16)))
         for b in range(2):
             c = 32 * (d % 4) + 16 * b
             mm(A("ps%d" % bank[d], c, c + 16), A("gt", 256 * d + 128 * b, 256 * d + 128 * b + 128), A("i16", 0, 16),
                True, True, "g_m%d" % bank[d])
-        if d == 3:
-            turn(A("s5", 0, 128), A("ps0", 0, 128))
-    turn(A("s5", 128, 224), A("ps1", 0, 96))
-    turn(A("land5", 32 * me, 32 * me + 32), A("ps2", 96, 128))
-    send("s5", 32, "land5", "arr5")
+        if d == 2:
+            turn(A("s5", 0, 64), A("ps0", 0, 64))
+    turn(A("s5", 64, 128), A("ps1", 64, 128))
+    turn(A("s5", 128, 160), A("ps1", 0, 32))
+    turn(A("s5", 160, 224), A("ps2", 32, 96))
+    turn(A("land5", 32 * me, 32 * me + 32), A("ps3", 96, 128))
+    send("s5", 32, "land5", "arr5", calls5)
     iota("w4", 2048, [[0, 2048]], 0, 0, True)
 
     ts(A("xbo"), A("pint"), 11, OPS.arith_shift_right)
@@ -377,8 +380,8 @@ def rank_program(g, core, T, topo):
     tt(A("u6"), A("u4"), A("u5"), OPS.add)
     cp("v", A("xaou"), A("u6"))
 
-    arrival("land5", 32, "arr5")
-    for q, k, u0, u1, e in ((p_far[0], 5, 0, 8, "v"), (p_far[1], 6, 0, 8, "s"), (p_own, 4, 0, 8, "v"),
+    arrival("land5", 32, "arr5", calls5)
+    for q, k, u0, u1, e in ((p_far0, 5, 0, 8, "v"), (p_own, 4, 0, 8, "s"), (p_far1, 6, 0, 8, "v"),
                             (p_near, 7, 0, 4, "s"), (p_near, 3, 4, 6, "v"), (p_near, 0, 6, 8, "s")):
         for u in range(u0, u1):
             h = 2 * (u % 4) + u // 4
@@ -387,37 +390,48 @@ def rank_program(g, core, T, topo):
         cp(e, A("ta", 256 * q + 64 * u0, 256 * q + 64 * u1), A("ps%d" % k, 0, 64 * (u1 - u0)))
     mm(A("ps2"), A("mbb"), A("exb"), True, True, "g_mb")
 
-    def sum_own(w, half, ps, grp):
-        for i in range(4):
-            for k in range(2):
-                lo = 1024 * k + 128 * (4 * half + i)
-                mm(A(ps, 32 * i + 16 * k, 32 * i + 16 * k + 16), A(w, lo, lo + 128), A("i16", 0, 16), True, True,
-                   "g_%s%d" % (grp, half))
+    def sum_a(half, ps):
+        for k in range(8):
+            lo = 1024 * half + 128 * k
+            mm(A(ps, k, 128, step=8), A("w2", lo, lo + 128), A("i16", 0, 16), True, True, "g_ya%d" % half)
 
-    def store(y, out, qs):
-        for h in range(8):
-            dma(qs[h % len(qs)], ext(T[out][:, 256 * h:256 * h + 256], "%s%d" % (out, h)),
-                A(y, 0, 256, 16 * h, 16 * h + 16), "d_" + out)
-
-    sum_own("w2", 0, "ps4", "ya")
+    sum_a(0, "ps4")
     tt(A("wb"), ind(A("ta"), A("xaou")), A("vcp"), OPS.mult)
     scan(A("rb"), A("ps2"), A("wb"))
     cp("v", ind(A("w3"), A("offb")), A("rb"))
-    turn(A("ya2", 0, 128), A("ps4", 0, 128))
+    cp("s", A("ya1", 0, 128), A("ps4", 0, 128))
 
     add_slabs("w3", "s6", "land6", "arr6")
-    sum_own("w2", 1, "ps5", "ya")
-    turn(A("ya2", 128, 256), A("ps5", 0, 128))
-    store("ya2", "ya", "y")
-    cp("v", A("lbu"), A("pl", 16, 32))
-    arrival("land6", 32, "arr6")
+
+    sum_a(1, "ps5")
+    cp("s", A("ya1", 128, 256), A("ps5", 0, 128))
+    for k in range(2):
+        mm(A("ps%d" % (6 + k), 0, 128), A("ya1", 128 * k, 128 * k + 128), A("ident"), True, True, "g_b%d" % k)
+        cp("s", A("ya2", 128 * k, 128 * k + 128), A("ps%d" % (6 + k), 0, 128))
+        dma("y", ext(T["ya"][:, 1024 * k:1024 * k + 1024], "ya%d" % k), A("ya2", 128 * k, 128 * k + 128), "d_ya")
+    ts(A("r1"), A("ln", 16, 32), 9, OPS.arith_shift_right)
+    ts(A("r2"), A("ln", 16, 32), 31, OPS.bitwise_and)
+    ts(A("r5"), A("ln", 16, 32), 4, OPS.mult)
+    ts(A("r3"), A("r1"), -2016, OPS.mult)
+    ts(A("r4"), A("r2"), -3, OPS.mult)
+    tt(A("r6"), A("r5"), A("r3"), OPS.add)
+    tt(A("lbu"), A("r6"), A("r4"), OPS.add)
+
+    arrival("land6", 32, "arr6", calls3)
     to_natural("land6", "q6", "ps2", "ps3")
     cp("v", ind(A("w4"), A("lbu")), A("q6"))
     for half in range(2):
-        sum_own("w4", half, "ps%d" % (6 + half), "yb")
-        turn(A("yb2", 128 * half, 128 * half + 128), A("ps%d" % (6 + half), 0, 128))
-    store("yb2", "yb", "ys")
-    record("y", None, [], [(None, [("ext_%s%d" % (n, h), 0, 128, 0, 1) for n in ("ya", "yb") for h in range(8)])])
+        ps = "ps%d" % half
+        for j in range(4):
+            for k in range(2):
+                lo = 1024 * k + 128 * (4 * half + j)
+                mm(A(ps, 32 * j + 16 * k, 32 * j + 16 * k + 16), A("w4", lo, lo + 128), A("i16", 0, 16), True, True,
+                   "g_yb%d" % half)
+        turn(A("yb2", 128 * half, 128 * half + 128), A(ps, 0, 128))
+    for h in range(8):
+        dma("ys"[h % 2], ext(T["yb"][:, 256 * h:256 * h + 256], "yb%d" % h), A("yb2", 0, 256, 16 * h, 16 * h + 16), "d_yb")
+    record("y", None, [], [(None, [("ext_ya%d" % h, 0, 128, 0, 1) for h in range(2)]
+                            + [("ext_yb%d" % h, 0, 128, 0, 1) for h in range(8)])])
 
     bits = [0] * len(ops)
     known = {}

import numpy as np
from concourse.bass import DstId, RemoteDMATransfer
from concourse.mybir import AluOpType, ActivationFunctionType

OPS = AluOpType
COPY = ActivationFunctionType.Copy
F, BFT, I32, U16, F16 = "float32", "bfloat16", "int32", "uint16", "float16"

NDUMP = 640
SCRATCH = {}
for _n, _c, _t in [
        ("i1", 128, I32), ("i1b", 128, I32), ("i2", 8, I32), ("i2b", 8, I32), ("i4", 128, I32),
        ("i4b", 128, I32), ("i5", 128, I32), ("ki", 32, I32), ("kk", 32, U16), ("dj", 32, F),
        ("mk", 8, F), ("i16", 512, F), ("z", 144, F), ("z16", 144, F16), ("ident", 128, F), ("mbf", 128, F),
        ("mbb", 128, BFT), ("e8", 128, F), ("n1", 128, F), ("n2", 128, F), ("p1", 128, F), ("p2", 128, F),
        ("repb", 1024, BFT), ("repf", 1024, F),
        ("tf", 2048, BFT), ("far", 2048, BFT), ("v8", 512, F), ("v16", 512, F), ("xi", 128, I32), ("ln", 32, I32),
        ("laf", 16, F), ("lau", 16, U16), ("lbu", 16, U16), ("lu", 32, U16), ("lf", 128, U16),
        ("xu", 64, U16), ("obu", 32, U16), ("xpa", 34, F), ("xpb", 34, F),
        ("r1", 16, I32), ("r2", 16, I32), ("r3", 16, I32), ("r4", 16, I32), ("r5", 16, I32), ("r6", 16, I32),
        ("ea", 32, F), ("ca", 32, F), ("da", 32, F), ("fma", 32, F), ("ga", 32, F), ("offa", 32, U16),
        ("eb", 32, F), ("cb2", 32, F), ("db", 32, F), ("fmb", 32, F), ("gb", 32, F), ("offb", 32, U16),
        ("exa", 512, BFT), ("exb", 512, BFT),
        ("pk0", 32, F), ("pk", 32, F), ("exp", 512, F), ("fp", 512, F), ("pm", 512, F), ("pm2", 256, F),
        ("pm4", 128, F), ("pm8", 64, F), ("pint", 32, I32),
        ("xao", 32, I32), ("xbo", 32, I32), ("u1", 32, I32), ("u2", 32, I32), ("u3", 32, I32), ("u4", 32, I32),
        ("u5", 32, I32), ("u6", 32, I32), ("xaou", 32, U16),
        ("s1", 512, BFT), ("land1", 512, BFT), ("tb", 2048, BFT), ("tc", 2048, BFT), ("vc", 512, F), ("vcp", 512, F),
        ("wa", 512, F), ("ra", 512, F), ("w1", 2048 + NDUMP, F), ("s3", 224, F), ("q3", 256, F), ("fan", 256, F),
        ("w2", 2048, F), ("gt", 2048, F), ("ya1", 256, F), ("ya2", 256, F),
        ("s5", 224, F), ("land3", 256, F), ("land5", 256, F), ("land6", 256, F), ("ta", 2048, F), ("wb", 512, F),
        ("rb", 512, F), ("w3", 2048 + NDUMP, F), ("s6", 224, F), ("q6", 256, F), ("w4", 2048, F), ("yb2", 256, F)]:
    SCRATCH[_n] = ("sbuf", [128, _c], _t)
SCRATCH["ll"] = ("sbuf", [128, 8, 4], I32)
SCRATCH["rr"] = ("sbuf", [128, 8, 8, 4], F16)
SCRATCH["rra"] = ("sbuf", [128, 128], F)
for _k in range(8):
    SCRATCH["ps%d" % _k] = ("psum", [128, 512], F)
NSEM = 130
SEMAPHORES = ["e%d" % k for k in range(NSEM)] + ["arr%d%s" % (k, s) for k in (1, 3, 5, 6) for s in "fhsn"] + ["sent"]


def rank_program(g, core, T, topo):
    me = T.rank_of(core)
    if me is None:
        return
    cores = list(T.cores)
    here = topo.chip(core)
    queues = {"v": g.vector, "s": g.scalar, "t": g.tensor, "g": g, "y": g.sync}

    ops = []
    hist = {}
    groups = {}

    def record(q, f, outs, ins, grp=None, inc=1, fixed=None):
        k = len(ops)
        dep = set()
        touched = []
        for w, side in ((1, outs), (0, ins)):
            for pair in side:
                for reg in pair[1]:
                    touched.append((w, reg))
        for w, reg in touched:
            n, a, b, lo, hi = reg
            for (j, w2, a2, b2, lo2, hi2) in hist.get(n, []):
                if n[:2] == "ps":
                    if ops[j]["q"] == q:
                        if q != "t" and (w or w2) and lo < hi2 and lo2 < hi:
                            dep.add(j)
                    else:
                        dep.add(j)
                elif (w or w2) and lo < hi2 and lo2 < hi and a < b2 and a2 < b:
                    dep.add(j)
        for w, reg in touched:
            hist.setdefault(reg[0], []).append((k, w) + tuple(reg[1:]))
        if grp is not None:
            groups.setdefault(grp, []).append(k)
        dep.discard(k)
        ops.append({"q": q, "f": f, "dep": dep, "grp": grp, "inc": inc, "fixed": fixed})
        return k

    def A(n, lo=0, hi=None, p0=0, p1=128, step=1):
        hi = SCRATCH[n][1][1] if hi is None else hi
        return (T[n][p0:p1, lo:hi] if step == 1 else T[n][p0:p1, lo:hi:step], [(n, p0, p1, lo, hi)])

    def X(ap, n, lo, hi):
        return (ap, [(n, 0, 128, lo, hi)])

    def ind(win, off):
        return (win[0].indirect(off[0]), win[1] + off[1])

    def cp(q, out, in_, grp=None):
        if q == "v":
            record(q, lambda: g.vector.tensor_copy(out[0], in_[0]), [out], [in_], grp)
        else:
            record(q, lambda: g.scalar.activation(out[0], in_[0], COPY), [out], [in_], grp)

    def scaled(out, in_, s, grp=None):
        record("s", lambda: g.scalar.activation(out[0], in_[0], COPY, scale=s[0]), [out], [in_, s], grp)

    def tt(out, a, b, o, grp=None):
        record("v", lambda: g.vector.tensor_tensor(out[0], a[0], b[0], o), [out], [a, b], grp)

    def ts(out, a, s1, o1, s2=None, o2=None, grp=None):
        ins = [a] + [s for s in (s1, s2) if isinstance(s, tuple)]
        v1 = s1[0] if isinstance(s1, tuple) else s1
        v2 = s2[0] if isinstance(s2, tuple) else s2
        if o2 is None:
            record("v", lambda: g.vector.tensor_scalar(out[0], a[0], v1, None, o1), [out], ins, grp)
        else:
            record("v", lambda: g.vector.tensor_scalar(out[0], a[0], v1, v2, o1, o2), [out], ins, grp)

    def fill(out, c, grp=None):
        record("v", lambda: g.vector.memset(out[0], c), [out], [], grp)

    def turn(out, in_):
        record("v", lambda: g.vector.transpose(out[0], in_[0]), [out], [in_])

    def mm(out, l, r, start, stop, grp):
        record("t", lambda: g.tensor.matmul(out[0], l[0], r[0], start, stop), [out], [l, r], grp)

    def iota(n, cols, pattern, base, cm, fl=False):
        out = A(n, 0, cols)
        if fl:
            record("g", lambda: g.iota(out[0], pattern, base, cm, allow_small_or_imprecise_dtypes=True), [out], [])
        else:
            record("g", lambda: g.iota(out[0], pattern, base, cm), [out], [])

    def pick(n, base):
        out, same = A(n), A("mbf")
        record("g", lambda: g.affine_select(out[0], same[0], [[-1, 128]], OPS.is_equal, 0.0, base, 1), [out], [same])

    def scan(out, keep, x):
        record("v", lambda: g.vector.tensor_tensor_scan(out[0], keep[0], x[0], 0.0, OPS.mult, OPS.add), [out], [keep, x])

    def dma(q, out, in_, grp, after=()):
        e = queues[q]
        record(q, lambda: e.dma_start(out[0], in_[0]), [out], [in_] + list(after), grp, 16)

    def ext(ap, n):
        return (ap, [("ext_" + n, 0, 128, 0, 1)])

    ranks = range(len(cores))

    def chip(q):
        return topo.chip(cores[q])

    def row(q):
        return len([p for p in ranks if p < q and topo.same_plane(chip(p), chip(q))])

    sib = [q for q in ranks if q != me and chip(q) == here]
    near = [q for q in ranks if topo.same_plane(chip(q), here)]
    others = [q for q in ranks if q != me and q not in sib and q not in near]
    far0 = [q for q in others if row(q) == row(me)]
    far1 = [q for q in others if q not in far0]
    order = far0 + far1 + sib + near + [me]
    p_own, p_far0, p_far1, p_near = min(sib + [me]), min(far0), min(far1), min(near)
    kinds = (("s", sib), ("f", far0), ("h", far1), ("n", near))

    off_chip = topo.engines(core, cores[others[0]])
    on_chip = [e for e in topo.engines(core, cores[sib[0]]) if e not in off_chip]

    def engines_for(q, dests):
        if q in sib:
            return on_chip[:len(on_chip) // 2]
        dests = [d for d in dests if d not in sib]
        n = len(off_chip) // len(dests)
        i = dests.index(q)
        return off_chip[i * n:(i + 1) * n]

    sent = [0]

    def send(src, width, dst, arr, calls):
        for dests in calls:
            tr, rd = [], []
            for q in dests:
                d = order.index(q)
                s = A(src, d * width, (d + 1) * width)
                rd.append(s)
                rid, pid = topo.addr(cores[q])[:2]
                es = engines_for(q, dests)
                sent[0] += len(es)
                w = [k for k, qs in kinds if q in qs][0]
                tr.append(RemoteDMATransfer(dst_ids=[DstId(rid=rid, pnc=pid)], dma_engine_mask=sum(1 << e for e in es),
                                            remote_sem=T.sem[arr + w], srcs=[s[0]],
                                            dsts=[T[dst][:, width * me:width * me + width]]))
            record("g", lambda tr=tr: g.remote_dma_fused(tr, local_sem=T.sem["sent"]), [], rd)

    def arrival(n, width, arr, calls):
        for w, srcs in kinds:
            regs = [(n, 0, 128, q * width, (q + 1) * width) for q in srcs]
            num = sum(len(engines_for(q, dests)) for dests in calls for q in dests if q in srcs)
            record("in_" + arr + w, None, [(None, regs)], [], fixed=(arr + w, num))

    calls1 = (far0 + far1, near + sib)
    calls3 = (far0, far1, near + sib)
    calls5 = (far0, far1 + sib, near)

    dma("y", X(T["ll"][:, 0:4, :], "ll", 0, 16), ext(T["lb"][:, :], "lb"), "d_l")
    dma("s", X(T["ll"][:, 4:8, :], "ll", 16, 32), ext(T["lc"][:, :], "lc"), "d_l")
    for k in range(8):
        n = "fb" if k < 4 else "fc"
        dma("ys"[k % 2], A("tf", 0, 2048, 16 * k, 16 * k + 16), ext(T[n][:, :], n), "d_tf")
    for k, n in enumerate(("xa", "xb", "xc", "ob")):
        dma("y", A("xi", 32 * k, 32 * k + 32), ext(T[n][:, :], n), "d_x")
    dma("y", A("v8", 0, 512, 0, 8), ext(T["v"][:, :], "v"), "d_x")
    dma("y", A("ln", 0, 16), ext(T["la"][:, :], "la"), "d_x")
    dma("y", A("ln", 16, 32), ext(T["lb"][:, :], "lb"), "d_x")

    iota("i2", 8, [[-16, 8]], 0, 1)
    iota("i1", 128, [[0, 8], [-1, 16]], 16, 1)
    iota("i4", 128, [[-16, 8], [0, 16]], 0, 1)
    iota("i5", 128, [[1, 8], [0, 16]], 0, -1)
    iota("dj", 32, [[16, 32]], 2048, 1, True)
    iota("ki", 32, [[1, 32]], 0, 0)
    fill(A("z"), 0.0)
    ts(A("i2b"), A("i2"), 4, OPS.arith_shift_right)
    ts(A("mk"), A("i2b"), 0, OPS.is_equal)
    ts(A("i1b"), A("i1"), 15, OPS.bitwise_and)
    ts(A("i16", 0, 128), A("i1b"), 0, OPS.is_equal)
    cp("v", A("z", 112, 128), A("i16", 0, 16))
    ts(A("i4b"), A("i4"), 4, OPS.arith_shift_right)
    cp("v", A("z16"), A("z"))
    ts(A("mbf"), A("i4b"), 0, OPS.is_equal)
    for n, k in (("n1", -1), ("n2", 15), ("p1", 1), ("p2", -15)):
        pick(n, k)
    for h in range(8):
        scaled(A("repb", 128 * h, 128 * h + 128), A("i16", 0, 128), A("mk", h, h + 1), "g_repb")

    for d in range(8):
        r = order[d]
        ts(X(T["rr"][:, :, d, :], "rr", d, d + 1), X(T["ll"][:, :, :], "ll", 0, 32), A("mk", r, r + 1), OPS.mult,
           grp="g_rr")
    for h in range(8):
        b = 32 * (h // 2)
        mm((T["ps4"][b:b + 32, 0:32], [("ps4", b, b + 32, 0, 32)]), A("z16", 112 - 16 * (h % 2), 144 - 16 * (h % 2)),
           X(T["rr"][:, h, :, :], "rr", 0, 8), h % 2 == 0, h % 2 == 1, "g_lt")
    fill(A("xpa"), -1.0)
    cp("v", A("mbb"), A("mbf"))
    cp("v", A("lu"), A("ps4", 0, 32))
    fill(A("xpb"), -1.0)
    cp("v", A("kk"), A("ki"))
    ts(A("e8"), A("i5"), 0, OPS.is_equal)
    cp("v", A("s1", 0, 256), ind(A("tf"), A("lu", 0, 16)))
    cp("s", A("s1", 256, 512), ind(A("tf"), A("lu", 16, 32)))
    send("s1", 64, "land1", "arr1", calls1)
    pick("ident", 0)
    iota("w1", 2048, [[0, 2048]], 0, 0, True)
    rep, zero = A("repf"), A("w1", 0, 1024)
    record("g", lambda: g.affine_select(rep[0], zero[0], [[-16, 8], [0, 8], [-1, 16]], OPS.not_equal, 1.0, 0, 1),
           [rep], [zero])
    iota("w2", 2048, [[0, 2048]], 0, 0, True)
    cp("s", A("land1", 64 * me, 64 * me + 64), A("s1", 448, 512))

    for k in range(1, 4):
        cp("s", A("i16", 128 * k, 128 * k + 128), A("i16", 0, 128), "g_i16")
    cp("v", A("xpa", 1, 33), A("xi", 0, 32))

    def shift(xp, ps, s):
        mm(A(ps, 0, 32), A("n1"), A(xp, 1, 33), True, False, "g_n" + s)
        mm(A(ps, 0, 32), A("n2"), A(xp, 2, 34), False, True, "g_n" + s)
        mm(A(ps, 32, 64), A("p1"), A(xp, 1, 33), True, False, "g_n" + s)
        mm(A(ps, 32, 64), A("p2"), A(xp, 0, 32), False, True, "g_n" + s)

    def ends(xp, ps, s, off):
        tt(A("e" + s), A(ps, 0, 32), A(xp, 1, 33), OPS.not_equal)
        tt(A("fm" + s), A("d" + s), A("e" + s), OPS.mult)
        tt(A("g" + s), A("fm" + s), A("dj"), OPS.add)
        cp("v", A(off), A("g" + s))

    def spread(out, x, grp):
        for i in range(16):
            scaled(A(out, i, 512, step=16), A(x), A("i16", i, i + 1), grp)

    shift("xpa", "ps7", "a")
    mm(A("ps5"), A("e8", 0, 128, 0, 8), A("v8", 0, 512, 0, 8), True, True, "g_v")
    ts(A("pk0"), A("xi", 32, 64), 2048, OPS.mult)
    tt(A("da"), A("xpa", 1, 33), A("dj"), OPS.subtract)
    tt(A("ca"), A("ps7", 32, 64), A("xpa", 1, 33), OPS.is_equal)
    cp("s", A("v16"), A("ps5"))
    ends("xpa", "ps7", "a", "offa")
    cp("v", A("xu"), A("xi", 32, 96))
    tt(A("exa"), ind(A("ca"), A("kk")), A("i16"), OPS.mult)
    tt(A("pk"), A("pk0"), A("xpa", 1, 33), OPS.add)
    cp("v", A("obu"), A("xi", 96, 128))
    cp("v", A("lau"), A("ln", 0, 16))
    cp("v", A("laf"), A("ln", 0, 16))

    arrival("land1", 64, "arr1", calls1)
    for k in range(8):
        dma("y", A("far", 0, 2048, 16 * k, 16 * k + 16), ext(T["fa"][:, :], "fa"), "d_fa",
            [A("land1", 64 * q, 64 * q + 64) for q in near])
    for f, q, n, k, e in ((1, p_own, 2, 0, "s"), (0, p_own, 2, 4, "v"), (1, p_far0, 2, 1, "s"),
                          (1, p_far1, 2, 2, "v"), (0, p_far0, 2, 5, "s"), (0, p_far1, 2, 6, "v"),
                          (1, p_near, 1, 3, "s"), (1, p_near + 1, 1, 0, "v"), (0, p_near, 2, 7, "s")):
        for i in range(4 * n):
            w = 128 * (4 * f + i % 4)
            lo = 64 * (q + i // 4)
            mm(A("ps%d" % k, 64 * i, 64 * i + 64), A("repb", w, w + 128), A("land1", lo, lo + 64), True, True,
               "g_t%d%d" % (k, q))
        cp(e, A("tb" if f == 0 else "tc", 256 * q, 256 * (q + n)), A("ps%d" % k, 0, 256 * n))
    mm(A("ps1"), A("mbb"), A("exa"), True, True, "g_ma")
    tt(A("vc"), ind(A("tc"), A("xu", 32, 64)), A("v16"), OPS.mult)
    tt(A("wa"), ind(A("tb"), A("xu", 0, 32)), A("vc"), OPS.mult)
    scan(A("ra"), A("ps1"), A("wa"))
    cp("v", ind(A("w1"), A("offa")), A("ra"))
    spread("exp", "pk", "g_exp")
    mm(A("ps2"), A("mbf"), A("exp"), True, True, "g_fp")
    cp("s", A("fp"), A("ps2"))
    cp("s", A("vcp"), ind(A("vc"), A("obu")))

    def add_slabs(w, s, land, arr):
        for qs, k in ((far0, 0), (far1, 1), (near + sib, 2), ([me], 3)):
            for q in qs:
                for b in range(2):
                    c = 32 * (order.index(q) % 4)
                    mm(A("ps%d" % k, c + b, c + 32, step=2), A(w, 256 * q + 128 * b, 256 * q + 128 * b + 128),
                       A("i16", 0, 16), True, True, "g_%s%d" % (w, k))
        cp("v", A(s, 0, 64), A("ps0", 0, 64))
        cp("v", A(s, 64, 128), A("ps1", 64, 128))
        cp("s", A(s, 128, 224), A("ps2", 0, 96))
        send(s, 32, land, arr, calls3)
        cp("s", A(land, 32 * me, 32 * me + 32), A("ps3", 96, 128))

    add_slabs("w1", "s3", "land3", "arr3")
    iota("w3", 2048, [[0, 2048]], 0, 0, True)

    cp("s", A("fan"), ind(A("far"), A("lau")))
    for d in range(8):
        r = order[d]
        scaled(A("rra", 16 * d, 16 * d + 16), A("laf"), A("mk", r, r + 1), "g_rra")
    mm(A("ps4", 0, 128), A("i16", 0, 128), A("rra"), True, True, "g_lf")
    tt(A("pm"), ind(A("fp"), A("obu")), A("i16"), OPS.mult)
    tt(A("pm2"), A("pm", 0, 512, step=2), A("pm", 1, 512, step=2), OPS.add)
    cp("v", A("lf"), A("ps4", 0, 128))
    tt(A("pm4"), A("pm2", 0, 256, step=2), A("pm2", 1, 256, step=2), OPS.add)
    tt(A("pm8"), A("pm4", 0, 128, step=2), A("pm4", 1, 128, step=2), OPS.add)
    tt(A("pint"), A("pm8", 0, 64, step=2), A("pm8", 1, 64, step=2), OPS.add)

    def to_natural(land, q, pa, pb):
        mm(A(pa, 0, 128), A(land, 0, 256, step=2), A("ident"), True, True, "g_n0" + land)
        mm(A(pb, 0, 128), A(land, 1, 256, step=2), A("ident"), True, True, "g_n1" + land)
        cp("s", A(q, 0, 128), A(pa, 0, 128))
        cp("v", A(q, 128, 256), A(pb, 0, 128))

    arrival("land3", 32, "arr3", calls3)
    to_natural("land3", "q3", "ps6", "ps7")
    tt(ind(A("w2"), A("lau")), A("q3"), A("fan"), OPS.mult)
    bank = (0, 0, 1, 1, 1, 2, 2, 3)
    for d in range(8):
        for lo, hi in ((0, 128), (128, 256)) if d < 2 else ((0, 256),):
            cp("vsvsvssv"[d], A("gt", 256 * d + lo, 256 * d + hi),
               ind(A("w2"), A("lf", 16 * d + lo // 16, 16 * d + hi // 16)))
        for b in range(2):
            c = 32 * (d % 4) + 16 * b
            mm(A("ps%d" % bank[d], c, c + 16), A("gt", 256 * d + 128 * b, 256 * d + 128 * b + 128), A("i16", 0, 16),
               True, True, "g_m%d" % bank[d])
        if d == 2:
            turn(A("s5", 0, 64), A("ps0", 0, 64))
    turn(A("s5", 64, 128), A("ps1", 64, 128))
    turn(A("s5", 128, 160), A("ps1", 0, 32))
    turn(A("s5", 160, 224), A("ps2", 32, 96))
    turn(A("land5", 32 * me, 32 * me + 32), A("ps3", 96, 128))
    send("s5", 32, "land5", "arr5", calls5)
    iota("w4", 2048, [[0, 2048]], 0, 0, True)

    ts(A("xbo"), A("pint"), 11, OPS.arith_shift_right)
    cp("v", A("xpb", 1, 33), A("xbo"))
    shift("xpb", "ps1", "b")
    ts(A("xao"), A("pint"), 2047, OPS.bitwise_and)
    tt(A("db"), A("xpb", 1, 33), A("dj"), OPS.subtract)
    tt(A("cb2"), A("ps1", 32, 64), A("xpb", 1, 33), OPS.is_equal)
    spread("exb", "cb2", "g_exb")
    ends("xpb", "ps1", "b", "offb")
    ts(A("u1"), A("xao"), 5, OPS.arith_shift_right, 7, OPS.bitwise_and)
    ts(A("u2"), A("xao"), 8, OPS.arith_shift_right, 1, OPS.bitwise_and)
    ts(A("u3"), A("u1"), 32, OPS.mult)
    ts(A("u4"), A("u2"), -224, OPS.mult)
    tt(A("u5"), A("u3"), A("xao"), OPS.add)
    tt(A("u6"), A("u4"), A("u5"), OPS.add)
    cp("v", A("xaou"), A("u6"))

    arrival("land5", 32, "arr5", calls5)
    for q, k, u0, u1, e in ((p_far0, 5, 0, 8, "v"), (p_own, 4, 0, 8, "s"), (p_far1, 6, 0, 8, "v"),
                            (p_near, 7, 0, 4, "s"), (p_near, 3, 4, 6, "v"), (p_near, 0, 6, 8, "s")):
        for u in range(u0, u1):
            h = 2 * (u % 4) + u // 4
            mm(A("ps%d" % k, 64 * (u - u0), 64 * (u - u0) + 64), A("repf", 128 * h, 128 * h + 128),
               A("land5", 32 * q, 32 * q + 64), True, True, "g_u%d" % k)
        cp(e, A("ta", 256 * q + 64 * u0, 256 * q + 64 * u1), A("ps%d" % k, 0, 64 * (u1 - u0)))
    mm(A("ps2"), A("mbb"), A("exb"), True, True, "g_mb")

    def sum_a(half, ps):
        for k in range(8):
            lo = 1024 * half + 128 * k
            mm(A(ps, k, 128, step=8), A("w2", lo, lo + 128), A("i16", 0, 16), True, True, "g_ya%d" % half)

    sum_a(0, "ps4")
    tt(A("wb"), ind(A("ta"), A("xaou")), A("vcp"), OPS.mult)
    scan(A("rb"), A("ps2"), A("wb"))
    cp("v", ind(A("w3"), A("offb")), A("rb"))
    cp("s", A("ya1", 0, 128), A("ps4", 0, 128))

    add_slabs("w3", "s6", "land6", "arr6")

    sum_a(1, "ps5")
    cp("s", A("ya1", 128, 256), A("ps5", 0, 128))
    for k in range(2):
        mm(A("ps%d" % (6 + k), 0, 128), A("ya1", 128 * k, 128 * k + 128), A("ident"), True, True, "g_b%d" % k)
        cp("s", A("ya2", 128 * k, 128 * k + 128), A("ps%d" % (6 + k), 0, 128))
        dma("y", ext(T["ya"][:, 1024 * k:1024 * k + 1024], "ya%d" % k), A("ya2", 128 * k, 128 * k + 128), "d_ya")
    ts(A("r1"), A("ln", 16, 32), 9, OPS.arith_shift_right)
    ts(A("r2"), A("ln", 16, 32), 31, OPS.bitwise_and)
    ts(A("r5"), A("ln", 16, 32), 4, OPS.mult)
    ts(A("r3"), A("r1"), -2016, OPS.mult)
    ts(A("r4"), A("r2"), -3, OPS.mult)
    tt(A("r6"), A("r5"), A("r3"), OPS.add)
    tt(A("lbu"), A("r6"), A("r4"), OPS.add)

    arrival("land6", 32, "arr6", calls3)
    to_natural("land6", "q6", "ps2", "ps3")
    cp("v", ind(A("w4"), A("lbu")), A("q6"))
    for half in range(2):
        ps = "ps%d" % half
        for j in range(4):
            for k in range(2):
                lo = 1024 * k + 128 * (4 * half + j)
                mm(A(ps, 32 * j + 16 * k, 32 * j + 16 * k + 16), A("w4", lo, lo + 128), A("i16", 0, 16), True, True,
                   "g_yb%d" % half)
        turn(A("yb2", 128 * half, 128 * half + 128), A(ps, 0, 128))
    for h in range(8):
        dma("ys"[h % 2], ext(T["yb"][:, 256 * h:256 * h + 256], "yb%d" % h), A("yb2", 0, 256, 16 * h, 16 * h + 16), "d_yb")
    record("y", None, [], [(None, [("ext_ya%d" % h, 0, 128, 0, 1) for h in range(2)]
                            + [("ext_yb%d" % h, 0, 128, 0, 1) for h in range(8)])])

    bits = [0] * len(ops)
    known = {}
    need = set()
    for k, o in enumerate(ops):
        have = known.get(o["q"], 0)
        waits = []
        for j in sorted(o["dep"], reverse=True):
            if have >> j & 1:
                continue
            members = groups[ops[j]["grp"]] if ops[j]["grp"] is not None else [j]
            if k in members:
                continue
            assert max(members) < k
            for m in members:
                have |= bits[m]
            waits.append(j)
            need.add(j)
        known[o["q"]] = have
        bits[k] = have | 1 << k
        o["waits"] = waits
        o["have"] = have
    needed_groups = set(ops[j]["grp"] for j in need if ops[j]["grp"] is not None)
    chains, used, place, group_sem = [], [0], {}, {}

    def fresh():
        used[0] += 1
        return "e%d" % (used[0] - 1)

    for k, o in enumerate(ops):
        if o["fixed"] is not None:
            place[k] = o["fixed"]
        elif o["grp"] in needed_groups and o["grp"] is not None:
            if o["grp"] not in group_sem:
                group_sem[o["grp"]] = fresh()
            place[k] = (group_sem[o["grp"]], sum(ops[m]["inc"] for m in groups[o["grp"]]))
        elif k in need:
            for c in chains:
                if c["q"] == o["q"] and o["have"] >> c["last"] & 1:
                    break
            else:
                c = {"q": o["q"], "sem": fresh(), "last": None, "n": 0}
                chains.append(c)
            c["last"] = k
            c["n"] += o["inc"]
            place[k] = (c["sem"], c["n"])
    assert used[0] <= NSEM, used[0]

    for k, o in enumerate(ops):
        if o["fixed"] is not None:
            continue
        q = queues[o["q"]]
        best = {}
        for j in o["waits"]:
            s, v = place[j]
            best[s] = max(v, best.get(s, 0))
        for s in sorted(best):
            q.wait_ge(T.sem[s], best[s])
        if o["f"] is None:
            continue
        x = o["f"]()
        if k in place:
            x.then_inc(T.sem[place[k][0]], o["inc"])
    g.wait_ge(T.sem["sent"], sent[0])
